import numpy as np, ml_dtypes
CORES = [2,3,42,43,82,83,122,123]
N = 8
BF = ml_dtypes.bfloat16
V, M, T = 512, 2, 6
WIN = N * V
HI = WIN // 16
B = V // M
H = (N, 8, 16, V)
def sized(u, hi):
    return np.where(u < 0, -1.0, 1.0) * np.clip(np.abs(u), 0.125, hi)
def draw(rng):
    return {"x": np.minimum((rng.random(H) * rng.choice(np.array([8, 16, 16, 24]), (N, 8, 1, V))).astype(np.int64), 15),
            "u": sized(rng.standard_normal(H, dtype=np.float32) * np.exp2(rng.integers(-1, 1, (N, 8, 16, 1))), 3.0),
            "w": (rng.random(H) * rng.choice(np.array([4, 8, 12, 16]), (N, 8, 1, V))).astype(np.int64),
            "ag": rng.choice(np.array([0, 1, 2, 3, 3, 3]), H), "s": rng.integers(0, WIN, H), "p": rng.integers(0, WIN, H),
            "j": rng.integers(0, HI, (N, 8, 16, WIN)), "tb": rng.integers(30, 110, (N, 8, 16)), "te": rng.integers(40, 200, (N, 8, 16))}
def pack(d):
    o = {}
    o["x0"] = d["x"].reshape(N, 128, V).astype(np.float32).astype(BF)
    o["u0"] = d["u"].reshape(N, 128, V).astype(np.float32)
    o["s0"] = d["s"].reshape(N, 128, V).astype(np.int32)
    o["p0"] = d["p"].reshape(N, 128, V).astype(np.int32)
    o["w0"] = d["w"].reshape(N, 128, V).astype(np.float32).astype(BF)
    o["ag"] = d["ag"].reshape(N, 128, V).astype(np.float32).astype(BF)
    o["ax"] = d["j"].reshape(N, 128, WIN).astype(np.float32).astype(BF)
    o["th"] = np.stack([d["tb"], d["te"]], axis=-1).reshape(N, 128, 2).astype(np.int32)
    return o
def ends(rng, lo, hi, shape, share):
    e = np.where(rng.random(shape) < 0.5, lo, hi)
    return np.where(rng.random(shape) < share, e, rng.integers(lo, hi + 1, shape))
def setup_inputs(rng):
    return pack(draw(rng))
def setup_inputs_spread(rng):
    d = draw(rng); c = (N, 8, 1, V)
    d["u"] = sized(d["u"] * np.exp2(rng.integers(-1, 2, c)), 8.0)
    d["x"] = np.minimum((np.exp2(4 * rng.random(H)) - 1).astype(np.int64) + rng.integers(0, 4, c), 15)
    d["w"] = np.minimum(np.exp2(4 * rng.random(H)).astype(np.int64), 15) * (rng.random(H) > 0.1)
    d["tb"] = rng.integers(0, 241, (N, 8, 16)); d["te"] = rng.integers(0, 241, (N, 8, 16))
    return pack(d)
def setup_inputs_ends(rng):
    d = draw(rng)
    d["x"] = ends(rng, 0, 15, H, 1.0)
    d["w"] = 15 * (rng.random(H) < rng.choice(np.array([0.0, 0.1, 0.2, 1.0]), (N, 8, 1, V))).astype(np.int64)
    d["ag"] = ends(rng, 0, 3, H, 0.8)
    d["s"] = ends(rng, 0, WIN - 1, H, 0.7); d["p"] = ends(rng, 0, WIN - 1, H, 0.7)
    d["j"] = ends(rng, 0, HI - 1, (N, 8, 16, WIN), 0.7)
    d["tb"] = ends(rng, 0, 240, (N, 8, 16), 0.8); d["te"] = ends(rng, 0, 240, (N, 8, 16), 0.8)
    d["u"] = np.where(rng.random(H) < 0.5, -1.0, 1.0) * np.where(rng.random(H) < 0.5, 0.125, 8.0)
    d["u"][:, ::2, :, V - 2:] = 8.0; d["u"][:, 1::2, :, V - 2:] = -8.0
    low = np.where(rng.permutation(8) < 4, 0, 15)[:, None, None]
    d["x"][0, :, :, :16] = low; d["w"][0, :, :, :16] = low
    d["x"][N - 1, :, :, V - 32:] = 15; d["w"][N - 1, :, :, V - 32:] = 15
    d["x"][:, :, :, V - 2:] = 15; d["w"][:, :, :, V - 2:] = 15
    d["ag"][:, :, :, V - 1] = 0; d["p"][:, :, :, V - 1] = WIN - 1
    d["ag"][:, :, :, V - 2] = 3; d["s"][:, :, :, V - 2] = WIN - 1
    d["x"][:, :, :, V - 3] = 0; d["w"][:, :, :, V - 3] = 0; d["ag"][:, :, :, V - 3] = 0
    d["te"][:, 7, 15] = 240; d["te"][:, 7, 0] = 0; d["tb"][:, 7, 15] = 240; d["tb"][:, 7, 0] = 0
    return pack(d)
def setup_inputs_corners(rng):
    d = draw(rng)
    lev = np.broadcast_to(rng.choice(np.array([0, 3, 6, 11, 15]), (N, 8, 1, V)), H)
    d["x"][:, ::2] = lev[:, ::2]
    many = rng.choice(np.array([0, 1, 2, 3, 4, 5, 6, 7, 8, 9, 15, 16]), (N, 8, 1, V))
    many[:, 3] = 16; many[::2, 4] = 0
    live = np.argsort(rng.random(H), axis=2) < many
    age = rng.integers(0, 3, H); age[:, 0] = 2; age[:, 1] = 0; age[:, 2] = 1
    d["ag"] = np.where(live, age, 3)
    d["w"] = rng.choice(np.array([0, 0, 0, 1, 1, 4, 11, 12, 15]), H)
    own = np.arange(N)[:, None, None, None] * V + np.arange(V)
    for k in ("s", "p"):
        c = rng.integers(0, 6, H)
        d[k] = np.where(c == 0, own, np.where(c == 1, 0, np.where(c == 2, WIN - 1, d[k])))
    for q in range(N):
        m = (8, 4, 0, 7, 1, 6, 3, 2)[q]
        d["te"][q] = np.where(rng.permutation(8) < m, 0, 240)[:, None]
    d["tb"] = rng.choice(np.array([0, 1, 60, 100, 239, 240]), (N, 8, 16))
    return pack(d)
def setup_inputs_crowd(rng):
    d = draw(rng); o = rng.permutation(8); z = rng.integers(0, WIN, 8); h = (N, 16, V)
    for i in range(4):
        g = int(o[i]); q = int(z[g]) // V; v = int(z[g]) % V
        d["s"][:, g] = z[g]; d["p"][:, g] = z[g]; d["ag"][:, g] = rng.integers(0, 3, h)
        d["x"][q, g, :, v] = rng.integers(4, 16, 16); d["w"][q, g, :, v] = 8
        if i >= 2:
            one = np.arange(16)[:, None] == rng.integers(0, 16, (N, 1, V))
            d["p"][:, g] = np.where(one, rng.integers(0, WIN, h), z[g]); d["s"][:, g] = np.where(one, rng.integers(0, WIN, h), z[g])
    g = int(o[4]); few = rng.integers(0, WIN, 4)
    d["s"][:, g] = rng.choice(few, h); d["p"][:, g] = rng.choice(few, h)
    keep = d["te"][1].copy(); d["te"][:] = 0; d["te"][:, int(o[7]), 1::2] = 240; d["te"][1] = keep
    return pack(d)
def setup_inputs_calm(rng):
    d = draw(rng); turn = int(rng.integers(0, 4))
    for q in range(N):
        d["te"][q] = np.where(rng.permutation(8) < q % 4, 0, 240)[:, None]
    d["ag"] = np.broadcast_to(((np.arange(8) + turn) % 4)[None, :, None, None], H).copy()
    lev = np.broadcast_to(rng.choice(np.array([3, 6, 9, 12]), (N, 8, 1, V)), H)
    d["x"][:, 1::2] = lev[:, 1::2]
    d["tb"] = rng.choice(np.array([0, 40, 80]), (N, 8, 16))
    return pack(d)
def check_ranges(d):
    bad = []
    for k, lo, hi in (("x0", 0, 15), ("s0", 0, WIN - 1), ("p0", 0, WIN - 1), ("w0", 0, 15), ("ag", 0, 3), ("ax", 0, HI - 1), ("th", 0, 240), ("u0", -8, 8)):
        v = np.asarray(d[k]).astype(np.float64)
        if not (np.min(v) >= lo and np.max(v) <= hi): bad.append("range of " + k)
        if k != "u0" and np.any(v != np.floor(v)): bad.append("whole numbers of " + k)
        if k == "u0" and not np.min(np.abs(v)) >= 0.125: bad.append("least size of " + k)
    return bad
def reference(x0, u0, s0, p0, w0, ag, ax, th):
    X, W, A = [a.astype(np.float32).astype(np.int64).reshape(H) for a in (x0, w0, ag)]
    S, P = [a.astype(np.int64).reshape(H) for a in (s0, p0)]
    U = u0.astype(np.float64).reshape(H); J = ax.astype(np.float32).astype(np.int64).reshape(N, 8, 16, WIN)
    tb = th[:, :, 0].astype(np.int64).reshape(N, 8, 16, 1); te = th[:, :, 1].astype(np.int64).reshape(N, 8, 16, 1)
    gi = np.arange(8)[:, None, None, None]; ii = np.arange(16)[None, :, None, None]; K = np.arange(16)[:, None]
    for t in range(T):
        a = (t % M) * B; b = a + B
        XA = X.transpose(1, 2, 0, 3).reshape(8, 16, WIN); UA = U.transpose(1, 2, 0, 3).reshape(8, 16, WIN)
        s = S[..., a:b]; p = P[..., a:b]; e = W[..., a:b]; age = A[..., a:b]
        live = age < 3
        C = np.where(live, p, s)
        w = e * (4 - np.where(live, age, 0))
        c = np.zeros((N, 8, 16, B), np.int64); sx = np.zeros((N, 8, 16, B), np.int64); su = np.zeros((N, 8, 16, B))
        for r in range(N):
            ix = C[r][:, None]; wr = w[r][:, None]
            XC = XA[gi, ii, ix]
            c[r] = np.sum(np.minimum(XC, X[r][:, :, None, a:b]), axis=1)
            sx[r] = np.sum(wr * XC, axis=2)
            su[r] = np.sum(wr * UA[gi, ii, ix], axis=2)
        nx = np.minimum(sx >> 8, 15)
        nu = np.tanh(su * 2.0 ** -11 + 0.5 * U[..., a:b] + 0.0625 * (X[..., a:b] - 8))
        strong = np.sum(nx, axis=2, keepdims=True) >= te
        n = np.sum(strong.astype(np.int64), axis=1, keepdims=True)
        key = np.where(live, 16 * c + 15 - K, -1)
        before = np.sum((key[:, :, :, None] > key[:, :, None]).astype(np.int64), axis=2)
        cap = live & strong & (before < n)
        fresh = ~live & (c >= tb)
        q = (C + 16 * np.take_along_axis(J, C, 3) + K) & (WIN - 1)
        s2 = np.where(cap, p, s); e2 = np.where(cap, np.minimum(e + 4, 15), e); p2 = np.where(fresh, q, p)
        a2 = np.where(cap, 3, np.where(live, age + 1, np.where(fresh, 0, 3)))
        S[..., a:b] = s2; W[..., a:b] = e2; P[..., a:b] = p2; A[..., a:b] = a2; X[..., a:b] = nx; U[..., a:b] = nu
    Y = np.where(A < 3, P, S)
    return {"yx": X.reshape(N, 128, V).astype(np.float32), "yu": U.reshape(N, 128, V).astype(np.float32), "yc": Y.reshape(N, 128, V).astype(np.float32), "yw": (16 * A + W).reshape(N, 128, V).astype(np.float32)}

def check_inputs(d):
    bad = list(check_ranges(d))
    if not bad:
        for name, y in reference(**d).items():
            for q in range(N):
                v = np.abs(np.asarray(y[q], np.float64)); s = np.sqrt(np.mean(v * v))
                if v.max() > 6 * s or s < 2.0 ** -3: bad.append('%s of rank %d is uneven or too small' % (name, q))
    return bad

@@ -1,0 +1,656 @@
+from concourse.bass import DstId, RemoteDMATransfer
+from concourse.mybir import AluOpType as ALU, ActivationFunctionType as ACT
+
+NV = 256
+SEQ = 2048
+SCAN = (1, 3)
+JENG = ("SSSS", "VVSS", "SSSS", "SSSS")
+
+F, BF, H, I32, U16 = "float32", "bfloat16", "float16", "int32", "uint16"
+IDN = {"one": 1.0, "p256": 256.0, "m3": -3.0, "p4": 4.0, "m1": -1.0, "p2": 2.0, "p3": 3.0, "p128": 128.0,
+       "m16": -16.0, "h0": 1792.0, "q0": -3840.0, "h1": -2304.0, "q1": 4352.0, "p32": 32.0, "m128": -128.0}
+IDK = list(IDN)
+SCRATCH = {
+    "XT": ("sbuf", [128, 7 * SEQ + NV], BF), "UT": ("sbuf", [128, 7 * SEQ + NV], F),
+    "AX": ("sbuf", [128, 4096], BF),
+    "GX": ("sbuf", [128, 4096], BF), "GU": ("sbuf", [128, 4096], F), "GJ": ("sbuf", [128, 4096], BF),
+    "GK": ("sbuf", [128, 4096], BF), "PM": ("sbuf", [128, 512], F),
+    "PX": ("sbuf", [128, 2048], H), "PU": ("sbuf", [128, 2048], F), "PS": ("sbuf", [128, 1024], F),
+    "MN": ("sbuf", [128, 1536], BF), "SD": ("sbuf", [128, 2048], BF),
+    "S0": ("sbuf", [128, 512], I32), "P0": ("sbuf", [128, 512], I32), "AG": ("sbuf", [128, 512], BF),
+    "TH": ("sbuf", [128, 4], I32), "QB": ("sbuf", [128, 8], F),
+    "WW": ("sbuf", [128, 2048], BF), "R4": ("sbuf", [128, 2048], BF), "NL": ("sbuf", [128, 1536 + 512], BF),
+    "LV": ("sbuf", [128, 512], BF), "WT": ("sbuf", [128, 1536], BF),
+    "CC": ("sbuf", [128, 2048], F), "GG": ("sbuf", [128, 1536], F), "D0": ("sbuf", [128, 512], F),
+    "DG": ("sbuf", [128, 512], F), "TT": ("sbuf", [128, 512], F), "N1": ("sbuf", [128, 512], F),
+    "TA": ("sbuf", [128, 256], F), "TB": ("sbuf", [128, 256], F),
+    "OF": ("sbuf", [128, 24, 64], U16), "OJ": ("sbuf", [128, 1024], U16),
+    "XP": ("sbuf", [128, 256], BF), "HQ": ("sbuf", [128, 512], BF),
+    "KEY": ("sbuf", [128, 256], BF), "FR": ("sbuf", [128, 256], BF), "CAP": ("sbuf", [128, 256], BF),
+    "STR": ("sbuf", [128, 256], BF), "OX": ("sbuf", [128, 256], F), "OW": ("sbuf", [128, 256], F),
+    "pI": ("sbuf", [128, 8], I32), "COL": ("sbuf", [128, 8], F), "rowm": ("sbuf", [128, 160], F),
+    "rowh": ("sbuf", [128, 128], F), "rowl": ("sbuf", [128, 128], F),
+    "ONE": ("sbuf", [128, 256], BF), "SEG": ("sbuf", [128, 512], F), "YY": ("sbuf", [128, 8, 32], BF),
+    "ID": ("sbuf", [128, 128 * len(IDK)], BF), "IH": ("sbuf", [128, 128], H), "IF": ("sbuf", [128, 256], F),
+    "KD": ("sbuf", [128, 128], BF), "BO": ("sbuf", [128, 128], BF), "ZZ": ("sbuf", [128, 144], BF),
+    "NM": ("sbuf", [128, 128], BF), "LM": ("sbuf", [128, 128], BF), "KM": ("sbuf", [128, 256], BF),
+    "MK": ("sbuf", [128, 32], F), "THR": ("sbuf", [128, 16], F),
+    "SW": ("sbuf", [128, 2048], BF), "DK": ("sbuf", [128, 2048], BF), "AD": ("sbuf", [128, 2048], BF),
+}
+for _b in range(8):
+    SCRATCH["B%d" % _b] = ("psum", [128, 512], F)
+NDMA = 20
+SEMAPHORES = (["cV", "cS", "cP", "cG", "sent"] + ["ax%d" % j for j in range(6)] + ["au%d" % j for j in range(6)]
+              + ["d%d" % j for j in range(NDMA)])
+
+CY, PC, GR, HOP = 0.00083, 0.00045, 1.5, 0.1
+ROUNDS, SEED, SHAKE = 15, 3, 0.3
+GXB = ("GX", "GX", "GJ", "GK", "GX", "GJ")
+ORDER = []
+LAT = {"xa": 7.5, "xb": 4.8, "ua": 9.0, "ub": 6.3, "x0": 14.0, "u0": 20.0}
+
+
+def span(shape, idx):
+    lo = hi = 0
+    n = 1
+    st = 1
+    for d in range(len(shape) - 1, 0, -1):
+        e = idx[d] if d < len(idx) else slice(None)
+        if isinstance(e, slice):
+            r = range(*e.indices(shape[d]))
+            lo += r[0] * st
+            hi += r[-1] * st
+            n *= len(r)
+        else:
+            lo += e * st
+            hi += e * st
+        st *= shape[d]
+    return lo, hi + 1, n
+
+
+def A(name, a=None, b=None, s=None):
+    return (name, (slice(None), slice(a, b, s)))
+
+
+def A3(name, a, b, c, d=None):
+    return (name, (slice(None), slice(a, b), c if d is None else slice(c, d)))
+
+
+def build(rank):
+    ops = []
+    hist = {}
+
+    def info(x):
+        where, shape, dt = SCRATCH[x[0]]
+        lo, hi, n = span(shape, x[1])
+        return where, lo, hi, n, dt
+
+    def add(eng, kind, args, reads, writes, cost, extra=(), lat=0.0):
+        i = len(ops)
+        deps = {}
+        for d in extra:
+            deps[d] = True
+        seen = set()
+        for x, w in [(x, True) for x in writes] + [(x, False) for x in reads]:
+            where, lo, hi, n, dt = info(x)
+            if where == "psum":
+                wr = any(y[0] == x[0] for y in writes)
+                rd = any(y[0] == x[0] for y in reads)
+                if x[0] in seen:
+                    continue
+                seen.add(x[0])
+                if x[0] in hist:
+                    j, jw = hist[x[0]]
+                    same = ops[j]["eng"] == eng
+                    need = not (same and (eng == "P" or (not jw and not wr)))
+                    deps[j] = deps.get(j, False) or need
+                hist[x[0]] = (i, wr)
+                continue
+            h = hist.setdefault(x[0], [])
+            keep = []
+            for e in h:
+                j, l2, h2, w2 = e
+                if j != i and l2 < hi and lo < h2 and (w or w2):
+                    deps[j] = True
+                if j != i and w and n == hi - lo and lo <= l2 and h2 <= hi:
+                    continue
+                keep.append(e)
+            keep.append((i, lo, hi, w))
+            hist[x[0]] = keep
+        if kind in ("load", "send", "iota"):
+            if (eng, kind != "load") in hist:
+                deps.setdefault(hist[eng, kind != "load"], False)
+            hist[eng, kind != "load"] = i
+        ops.append({"eng": eng, "kind": kind, "args": args, "deps": deps, "cost": cost, "lat": lat})
+        return i
+
+    def isap(x):
+        return isinstance(x, tuple)
+
+    def two(*xs):
+        return all(info(x)[4] in (BF, H, U16) for x in xs)
+
+    def vc(n):
+        return 0.05 + max(64, n) * CY
+
+    def ts(out, in0, s1, s2, op0, op1=None):
+        n = info(out)[3]
+        return add("V", "ts", (out, in0, s1, s2, op0, op1), [in0] + [s for s in (s1, s2) if isap(s)], [out],
+                   vc(n * (0.5 if two(out, in0) else 1)))
+
+    def tt(out, a, b, op):
+        n = info(out)[3]
+        return add("V", "tt", (out, a, b, op), [a, b], [out],
+                   vc(n * (2 if info(a)[0] == "sbuf" and info(b)[0] == "sbuf" else 1)))
+
+    def cp(out, a):
+        return add("V", "cp", (out, a), [a], [out], vc(info(out)[3] * (0.5 if two(out, a) else 1)))
+
+    def ms(out, c):
+        return add("V", "ms", (out, c), [], [out], vc(info(out)[3] * 0.5))
+
+    def scan(out, a, b):
+        return add("V", "scan", (out, a, b), [a, b], [out], vc(info(out)[3]))
+
+    def act(out, a, f, bias=0.0, scale=1.0):
+        return add("S", "act", (out, a, f, bias, scale), [a] + [s for s in (bias, scale) if isap(s)], [out],
+                   0.065 + max(64, info(out)[3]) * CY)
+
+    def gat(eng, out, win, off, extra=()):
+        return add(eng, "gat", (out, win, off), [win, off], [out], 0.06 + info(out)[3] * GR * CY, extra)
+
+    def mm(out, l, r, st=True, sp=True):
+        return add("P", "mm", (out, l, r, st, sp), [l, r], [out],
+                   max(64, info(out)[3]) * PC * (4 if info(r)[4] == F else 1))
+
+    def lin(out, terms):
+        for j, (l, r) in enumerate(terms):
+            mm(out, l, r, j == 0, j == len(terms) - 1)
+
+    def load(q, out, name, a, b, lat):
+        return add(q, "load", (out, name, a, b), [], [out], 0.1, lat=lat)
+
+    def store(name, a, b, src):
+        return add("Y", "store", (src, name, a, b), [src], [], 0.1, lat=2.0)
+
+    def idn(k):
+        j = IDK.index(k)
+        return A("ID", 128 * j, 128 * j + 128)
+
+    def own(j, a=0, b=NV):
+        o = j * SEQ + (rank * NV if j < 7 else 0)
+        return o + a, o + b
+
+    def send(tab, j, a, b, via, sem, lat):
+        lo, hi = own(j, a, b)
+        return add("G", "send", (tab, lo, hi, via, sem), [A(tab, lo, hi)], [], 0.5, lat=lat)
+
+    def arr(sem, sends):
+        return add("A", "arr", (sem,), [], [], 0.0, extra=sends)
+
+    def st(name, stage, b, a=0, e=NV):
+        o = stage * 512 + b * NV
+        return A(name, o + a, o + e)
+
+    for b in range(2):
+        load("YS"[b], A("XT", *own(b)), "x0", b * NV, b * NV + NV, 2.2)
+    load("Y", A("S0"), "s0", 0, 512, 2.6)
+    load("S", A("P0"), "p0", 0, 512, 2.8)
+    load("Y", A("AG"), "ag", 0, 512, 3.0)
+    load("S", A("WW", 0, 512), "w0", 0, 512, 3.2)
+    load("Y", A("TH", 0, 2), "th", 0, 2, 3.2)
+    for b in range(2):
+        load("SY"[b], A("UT", *own(b)), "u0", b * NV, b * NV + NV, 3.8)
+    load("Y", A("AX"), "ax", 0, 4096, 7.0)
+    add("G", "iota", (A("pI", 0, 1), [[0, 1]], 0, 1, False), [], [A("pI", 0, 1)], 0.14)
+    add("G", "iota", (A("rowm"), [[1, 160]], 0, 0, True), [], [A("rowm")], 0.4)
+    add("G", "iota", (A("rowh"), [[16, 8], [0, 16]], 0, 0, True), [], [A("rowh")], 0.35)
+    add("G", "iota", (A("rowl"), [[0, 8], [1, 16]], 0, 0, True), [], [A("rowl")], 0.35)
+    arrx = {0: arr("ax0", [send("XT", 0, 0, NV, True, "ax0", LAT["x0"]), send("XT", 1, 0, NV, False, "ax0", LAT["x0"] - 2)])}
+    arru = {0: arr("au0", [send("UT", 0, 0, NV, True, "au0", LAT["u0"]), send("UT", 1, 0, NV, False, "au0", LAT["u0"] - 2)])}
+
+    pc, kc, gc = A("COL", 0, 1), A("COL", 1, 2), A("COL", 2, 3)
+    ms(A("ONE"), 1.0)
+    ts(A("pI", 1, 2), A("pI", 0, 1), 15, None, ALU.bitwise_and)
+    ts(A("pI", 2, 3), A("pI", 0, 1), 112, None, ALU.bitwise_and)
+    cp(A("COL", 0, 3), A("pI", 0, 3))
+    ts(idn("one"), A("rowm", 0, 128), pc, None, ALU.is_equal)
+    ts(A("COL", 3, 4), pc, 8.0, None, ALU.add)
+    ts(A("COL", 4, 5), pc, -8.0, None, ALU.add)
+    ts(A("COL", 5, 6), kc, 8.0, None, ALU.is_lt)
+    ts(A("COL", 6, 7), kc, 8.0, None, ALU.is_ge)
+    for j, c in enumerate((0, 3, 4, 0)):
+        ts(A("PM", 128 * j, 128 * j + 128), A("rowm", 0, 128), A("COL", c, c + 1), A("COL", 5 + j // 2, 6 + j // 2),
+           ALU.is_equal, ALU.mult)
+    for k in IDK[1:]:
+        ts(idn(k), idn("one"), IDN[k], None, ALU.mult)
+    ts(A("IH"), idn("one"), 1.0 / 256, None, ALU.mult)
+    ts(A("IF", 0, 128), idn("one"), 1.0, None, ALU.mult)
+    ts(A("IF", 128, 256), idn("one"), 1024.0, None, ALU.mult)
+    ts(A("KD"), idn("one"), kc, None, ALU.mult)
+    ts(A("BO"), A("rowh"), gc, None, ALU.is_equal)
+    ts(A("ZZ"), A("rowm", 0, 144), -15.0, gc, ALU.add, ALU.is_equal)
+    ts(A("MK", 0, 16), A("rowm", 0, 16), kc, None, ALU.is_equal)
+    ts(A("MK", 16, 32), A("MK", 0, 16), 16.0, None, ALU.mult)
+    for k in range(16):
+        ts(A("SW", 128 * k, 128 * k + 128), A("BO"), A("MK", k, k + 1), None, ALU.mult)
+    for k in range(16):
+        act(A("DK", 128 * k, 128 * k + 128), idn("one"), ACT.Identity, 0.0, A("MK", 16 + k, 17 + k))
+    ts(A("KM", 0, 128), A("rowl"), kc, None, ALU.is_equal)
+    tt(A("NM"), A("KM", 0, 128), idn("p32"), ALU.add)
+    ts(A("KM", 128, 256), A("BO"), 2.0, None, ALU.mult)
+    tt(A("LM"), A("KM", 128, 256), idn("m128"), ALU.add)
+    ts(A("THR", 8, 16), A("rowm", 1, 9), kc, 16.0, ALU.add, ALU.is_ge)
+    ts(A("THR", 0, 8), A("THR", 8, 16), -0.5, None, ALU.add)
+    cp(A("QB", 0, 2), A("TH", 0, 2))
+    ts(A("QB", 2, 3), A("QB", 0, 1), 16.0, None, ALU.add)
+    ts(A("QB", 3, 4), A("QB", 1, 2), -1.0, 0.5, ALU.mult, ALU.add)
+    if SCAN:
+        ms(A("SEG"), 1.0)
+        ms(A("SEG", 0, 512, 8), 0.0)
+    yall = A3("YY", 0, 8, 0, 32)
+    j = add("G", "sel", (yall, A("ONE"), [[-16, 8], [0, 2], [-1, 16]], ALU.is_equal, 0.0), [A("ONE")], [yall], 0.6)
+    ops[j]["deps"][hist["G", True]] = False
+    for d in list(range(1, 16)):
+        o, y = A("AD", 128 * d, 128 * d + 128), A3("YY", 0, 8, d, d + 16)
+        add("G", "sel", (o, y, [[-1, 128]], ALU.not_equal, -1.0), [y], [o], 0.39)
+
+    def ad(d):
+        return A("AD", 128 * d, 128 * d + 128)
+
+    def columns(stage, b):
+        c = st("CC", stage, b)
+        act(A("HQ", 0, 256), c, ACT.Identity, 191.501953125, 1.0 / 256)
+        act(A("HQ", 256, 512), c, ACT.Identity, 191.5009765625, 1.0 / 512)
+        p = A("B4", 256, 512)
+        lin(p, [(idn("h%d" % b), A("HQ", 0, 256)), (idn("q%d" % b), A("HQ", 256, 512))])
+        tt(A("TB"), p, c, ALU.add)
+        j = 8 * stage + 4 * b
+        for hk in range(2):
+            lin(A("B4", 256 + 128 * hk, 384 + 128 * hk),
+                [(A("PM", 256 * hk + 128 * h, 256 * hk + 128 * h + 128), A("TB", h, 256, 2)) for h in range(2)])
+        for hk in range(2):
+            ts(A3("OF", j, j + 4, 32 * hk, 32 * hk + 32), A("B4", 256 + 128 * hk, 384 + 128 * hk),
+               393216.0 if b == 0 else 2048.0 - 393216.0, None, ALU.add)
+
+    def weights(stage, b):
+        p = A("B7", 256, 512)
+        lin(p, [(idn("one"), st("R4", stage, b)), (idn("p3"), st("NL", stage, b))])
+        tt(st("WT", stage, b), p, st("WW", stage, b), ALU.mult)
+
+    def start(b):
+        ag = st("AG", 0, b)
+        ts(st("LV", 0, b), ag, 3.0, None, ALU.is_lt)
+        p = A("B7", 0, 256)
+        tt(p, st("P0", 0, b), st("S0", 0, b), ALU.subtract)
+        tt(p, p, st("LV", 0, b), ALU.mult)
+        tt(st("CC", 0, b), p, st("S0", 0, b), ALU.add)
+        act(st("TT", 0, b), p, ACT.Identity)
+        cp(st("OJ", 0, b), st("CC", 0, b))
+        columns(0, b)
+        ts(st("NL", 0, b), ag, 3.0, None, ALU.is_equal)
+        ts(st("R4", 0, b), ag, -1.0, 4.0, ALU.mult, ALU.add)
+        weights(0, b)
+
+    def jump(rnd, b):
+        n = st("CC", 0, b) if rnd == 0 else st("N1", 0, b)
+        gj = "GJ" if b == 0 else "GK"
+        for ch in range(4):
+            gat(JENG[2 * rnd + b][ch], A(gj, 1024 * ch, 1024 * ch + 1024), A("AX"), st("OJ", rnd, b, 64 * ch, 64 * ch + 64))
+        p = A("B6", 0, 256)
+        lin(p, [(A("KD"), A("ONE"))] + [(A("DK", 128 * k, 128 * k + 128), A(gj, k, 4096, 16)) for k in range(16)])
+        tt(A("TA"), p, n, ALU.add)
+        ts(A("TB"), A("TA"), 4096.0, -4096.0, ALU.is_ge, ALU.mult)
+        if rnd == 0:
+            tt(st("GG", 0, b), p, A("TB"), ALU.add)
+            q = A("B6", 256, 512)
+            mm(q, idn("one"), st("NL", 0, b))
+            tt(q, q, st("GG", 0, b), ALU.mult)
+            tt(st("N1", 0, b), q, st("S0", 0, b), ALU.add)
+            tt(st("D0", 0, b), q, st("TT", 0, b), ALU.subtract)
+            cp(st("OJ", 1, b), st("N1", 0, b))
+        else:
+            tt(p, p, A("TB"), ALU.add)
+            tt(st("DG", 0, b), p, st("GG", 0, b), ALU.subtract)
+
+    ring = [0, 0, 0]
+
+    def products(t, tab, gbuf, pbuf, first):
+        b, s = t % 2, t // 2
+        for ch in range(4):
+            v = 64 * ch
+            gat("S", A(gbuf, 16 * v, 16 * v + 1024), A(tab, t * SEQ, t * SEQ + 2 * SEQ),
+                ("OF", (slice(None), 8 * s + 4 * b + ch)), first)
+            for hk in range(2):
+                bank = "B%d" % (ring[0] % 2)
+                ring[0] += 1
+                for kk in range(8):
+                    k = 8 * hk + kk
+                    mm(A(bank, kk, 512, 8), A("SW", 128 * k, 128 * k + 128), st("WT", s, b, v, v + 64))
+                o = 512 * ((2 * ch + hk) % 4)
+                tt(A(pbuf, o, o + 512), A(gbuf, 16 * v + 512 * hk, 16 * v + 512 * hk + 512), A(bank), ALU.mult)
+                yield ch, hk, o
+
+    def xphase(t):
+        sends = []
+        for ch, hk, o in products(t, "XT", GXB[t], "PX", [arrx[t]] if t in arrx else []):
+            v = 64 * ch
+            for kk in range(8):
+                mm(A("B3", v, v + 64), A("IH"), A("PX", o + kk, o + 512, 8), hk == 0 and kk == 0, hk == 1 and kk == 7)
+            if hk == 1 and ch % 2 == 1:
+                a = v - 64
+                ts(A("XP", a, a + 128), A("B3", a, a + 128), 15.0, 191.501953125, ALU.min, ALU.add)
+                ts(A("XT", *own(t + 2, a, a + 128)), A("XP", a, a + 128), -192.0, None, ALU.add)
+                if t < 5:
+                    sends.append(send("XT", t + 2, a, a + 128, a == 0, "ax%d" % (t + 1), LAT["xa" if a == 0 else "xb"]))
+        if t < 5:
+            arrx[t + 1] = arr("ax%d" % (t + 1), sends)
+        if t >= 4:
+            b = t % 2
+            act(A("OX"), A("XT", *own(t + 2)), ACT.Identity)
+            store("yx", b * NV, b * NV + NV, A("OX"))
+        mm(A("B3", 256, 512), A("BO"), A("XT", *own(t + 2)))
+        act(A("STR"), A("B3", 256, 512), ACT.Sign, A("QB", 3, 4))
+
+    def overlap(t):
+        b, s = t % 2, t // 2
+        for ch in range(4):
+            a = 64 * ch
+            bank = "B2" if ch % 2 == 0 else "B6"
+            for kk in range(8):
+                mm(A(bank, kk, 512, 8), idn("one"), A("XT", *own(t, a, a + 64)))
+            mm(A("B5", a, a + 64), idn("p256"), st("NL", s, b, a, a + 64), True, False)
+            for hk in range(2):
+                o = 512 * (ring[1] % 3)
+                ring[1] += 1
+                tt(A("MN", o, o + 512), A(GXB[t], 16 * a + 512 * hk, 16 * a + 512 * hk + 512), A(bank), ALU.min)
+                for kk in range(8):
+                    k = 8 * hk + kk
+                    mm(A("B5", a, a + 64), A("ZZ", 15 - k, 143 - k), A("MN", o + kk, o + 512, 8), False, k == 15)
+        act(A("KEY"), A("B5", 0, 256), ACT.Identity, -240.0)
+        ts(A("FR"), A("KEY"), A("QB", 2, 3), None, ALU.is_ge)
+
+    def uphase(t):
+        sends = []
+        for ch, hk, o in products(t, "UT", "GU", "PU", [arru[t]] if t in arru else []):
+            v = 64 * ch
+            bank = "B4" if ch < 2 else "B3"
+            r = A(bank, v % 128, v % 128 + 64)
+            if hk == 0:
+                mm(r, idn("p128"), A("XT", *own(t, v, v + 64)), True, False)
+                mm(r, A("IF", 128, 256), A("UT", *own(t, v, v + 64)), False, False)
+            if ch in SCAN:
+                scan(A("PS", 512 * hk, 512 * hk + 512), A("SEG"), A("PU", o, o + 512))
+                mm(r, A("IF", 0, 128), A("PS", 512 * hk + 7, 512 * hk + 512, 8), False, hk == 1)
+            else:
+                for kk in range(8):
+                    mm(r, A("IF", 0, 128), A("PU", o + kk, o + 512, 8), False, hk == 1 and kk == 7)
+            if hk == 1 and ch % 2 == 1:
+                a = v - 64
+                act(A("UT", *own(t + 2, a, a + 128)), A(bank, 0, 128), ACT.Tanh, -0.5, 2.0 ** -11)
+                if t < 5:
+                    sends.append(send("UT", t + 2, a, a + 128, a == 0, "au%d" % (t + 1), LAT["ua" if a == 0 else "ub"]))
+        if t < 5:
+            arru[t + 1] = arr("au%d" % (t + 1), sends)
+        if t >= 4:
+            b = t % 2
+            store("yu", b * NV, b * NV + NV, A("UT", *own(t + 2)))
+
+    def update(t):
+        b, s = t % 2, t // 2
+        nl, nn = st("NL", s, b), st("NL", s + 1, b)
+        for j in range(4):
+            bank = "B6" if j % 2 == 0 else "B2"
+            for e in range(2):
+                mm(A(bank, 256 * e, 256 * e + 256), ad(2 * j + e + 1), A("KEY"))
+            for e in range(2):
+                d = 2 * j + e
+                act(A("SD", 256 * d, 256 * d + 256), A(bank, 256 * e, 256 * e + 256), ACT.Sign, A("THR", d, d + 1))
+        z = A("B5", 256, 512)
+        lin(z, [(A("LM"), nl), (A("NM"), A("STR"))]
+            + [(ad(15 - d) if d < 7 else idn("m1"), A("SD", 256 * d, 256 * d + 256)) for d in range(8)])
+        ts(A("CAP"), z, 40.0, None, ALU.is_gt)
+        p, q = A("B7", 0, 256), A("B7", 256, 512)
+        lin(p, [(idn("one"), st("R4", s, b)), (idn("p4"), A("FR")), (idn("m3"), A("CAP"))])
+        lin(q, [(idn("one"), st("WW", s, b)), (idn("p4"), A("CAP"))])
+        ts(st("R4", s + 1, b), p, -1.0, 1.0, ALU.add, ALU.max)
+        ts(st("WW", s + 1, b), q, 15.0, None, ALU.min)
+        ts(nn, st("R4", s + 1, b), 1.0, None, ALU.is_equal)
+        c, cn, d0 = st("CC", s, b), st("CC", s + 1, b), st("D0", 0, b)
+
+        def ended(out, f):
+            lin(out, [(idn("m1"), nl), (idn(f), A("FR")), (idn("m1"), A("CAP")), (idn("one"), nn)])
+        u, w = A("B5", 0, 256), A("B5", 256, 512)
+        if s == 0:
+            ended(u, "p2")
+            tt(w, u, d0, ALU.mult)
+            tt(cn, w, c, ALU.add)
+        else:
+            mm(p, idn("one"), A("FR"))
+            ended(w, "one")
+            if s == 1:
+                ended(u, "p2")
+            tt(p, p, st("GG", s, b), ALU.mult)
+            tt(A("TA"), p, c, ALU.add)
+            tt(w, w, d0, ALU.mult)
+            tt(cn, w, A("TA"), ALU.add)
+        if s < 2:
+            columns(s + 1, b)
+            weights(s + 1, b)
+            tt(u, u, st("DG", 0, b), ALU.mult)
+            tt(st("GG", s + 1, b), u, st("GG", s, b), ALU.add)
+        else:
+            store("yc", b * NV, b * NV + NV, cn)
+            lin(p, [(idn("m16"), st("R4", 3, b)), (idn("one"), st("WW", 3, b))])
+            act(A("OW"), p, ACT.Identity, 64.0)
+            store("yw", b * NV, b * NV + NV, A("OW"))
+
+    start(0)
+    start(1)
+    jump(0, 0)
+    jump(0, 1)
+    for t in range(6):
+        xphase(t)
+        overlap(t)
+        if t < 2:
+            jump(1, t)
+        uphase(t)
+        update(t)
+    return ops
+
+
+def schedule(ops):
+    n = len(ops)
+    succ = [[] for _ in range(n)]
+    for i, o in enumerate(ops):
+        for d in o["deps"]:
+            succ[d].append(i)
+    lev = [0.0] * n
+    for i in range(n - 1, -1, -1):
+        o = ops[i]
+        lev[i] = o["cost"] + max([lev[j] + (o["lat"] + HOP if ops[j]["deps"][i] else 0.0) for j in succ[i]] + [o["lat"]])
+    gap = [dict((d, ops[d]["lat"] + HOP if w else 0.0) for d, w in o["deps"].items()) for o in ops]
+    back = [dict((j, gap[j][i]) for j in succ[i]) for i in range(n)]
+
+    def place(before, after, first, prio):
+        left = [len(b) for b in before]
+        rdy = list(first)
+        pool = dict((o["eng"], []) for o in ops)
+        for i in range(n):
+            if left[i] == 0:
+                pool[ops[i]["eng"]].append(i)
+        free = dict((e, 0.0) for e in pool)
+        end, order = [0.0] * n, []
+        while len(order) < n:
+            t, e = min((max(free[e], min(rdy[i] for i in pool[e])), e) for e in pool if pool[e])
+            i = min((j for j in pool[e] if rdy[j] <= t + 1e-9), key=lambda j: prio[j])
+            pool[e].remove(i)
+            order.append(i)
+            free[e] = end[i] = t + ops[i]["cost"]
+            for j, w in after[i].items():
+                rdy[j] = max(rdy[j], end[i] + w)
+                left[j] -= 1
+                if left[j] == 0:
+                    pool[ops[j]["eng"]].append(j)
+        return end, order
+
+    zero, tail = [0.0] * n, [o["lat"] if o["kind"] == "store" else 0.0 for o in ops]
+    best, r = None, SEED
+    for _ in range(ROUNDS):
+        end, order = place(gap, back, zero, [(-lev[i], i) for i in range(n)])
+        length = max(end[i] + tail[i] for i in range(n))
+        if best is None or length < best[0]:
+            best = (length, order)
+        lev = place(back, gap, tail, [(-end[i], -i) for i in range(n)])[0]
+        for i in range(n):
+            r = (r * 1103515245 + 12345) % 2147483648
+            lev[i] += SHAKE * r / 2147483648
+    ops[0]["span"] = best[0]
+    return best[1]
+
+
+COMPUTE = ("ts", "tt", "cp", "ms", "scan", "act", "gat", "mm", "iota", "sel")
+
+
+def routes(T, topo):
+    helper = {}
+    for c in T.cores:
+        for h in topo.cores_of(c):
+            if (h not in T.cores and h not in helper.values() and topo.die(h) != topo.die(c)
+                    and all(topo.may_write(h, d) for d in T.cores)):
+                helper[c] = h
+                break
+    return helper
+
+
+def spread(g, T, topo, src, dsts, ap, sem):
+    far = [d for d in dsts if topo.chip(d) != topo.chip(src)]
+    near = [d for d in dsts if d not in far]
+    outer = topo.mask(src, [c for c in T.cores if topo.chip(c) != topo.chip(src)][0])
+    tr = []
+    for ds in (far, near):
+        if ds:
+            m = outer if ds is far else topo.mask(src, ds[0]) & ~outer
+            tr.append(RemoteDMATransfer(dst_ids=[DstId(rid=topo.addr(d)[0], pnc=topo.addr(d)[1]) for d in ds],
+                                        dma_engine_mask=m, remote_sem=sem, srcs=[ap], dsts=[ap] * len(ds)))
+    g.remote_dma_fused(tr, local_sem=T.sem.sent)
+    return sum(bin(t_m).count("1") for t_m in ([outer] if far else []) + ([topo.mask(src, near[0]) & ~outer] if near else []))
+
+
+def rank_program(g, core, T, topo):
+    helper = routes(T, topo)
+    rank = T.rank_of(core)
+    owner = [c for c in helper if helper[c] == core]
+    if rank is None and not owner:
+        return
+    me = core if rank is not None else owner[0]
+    others = [c for c in T.cores if c != me]
+    ops = build(T.rank_of(me))
+    if not ORDER:
+        ORDER.extend(schedule(ops))
+    order = ORDER
+    far1 = [c for c in T.cores if topo.chip(c) != topo.chip(me)][0]
+    unit = len(topo.engines(me, far1))
+    if rank is None:
+        total = 0
+        for i in order:
+            if ops[i]["kind"] == "send" and ops[i]["args"][3]:
+                tab, lo, hi, via, sem = ops[i]["args"]
+                g.wait_ge(T.sem[sem], unit)
+                total += spread(g, T, topo, core, others, T[tab][:, lo:hi], T.sem[sem])
+        g.wait_ge(T.sem.sent, total)
+        return
+
+    pos, cnt, chan = {}, {}, {}
+    nd = 0
+    for i in order:
+        o = ops[i]
+        if o["kind"] in COMPUTE:
+            chan[i] = o["eng"]
+        elif o["kind"] in ("load", "store"):
+            chan[i] = "d%d" % nd
+            nd += 1
+        else:
+            chan[i] = o["args"][-1] if o["kind"] == "arr" else None
+        cnt[chan[i]] = cnt.get(chan[i], 0) + 1
+        pos[i] = cnt[chan[i]]
+    known = dict((e, {}) for e in "VSPGYA")
+    clock, waits, marked = {}, {}, set()
+    where = dict((i, n) for n, i in enumerate(order))
+    for i in order:
+        o = ops[i]
+        kn = known[o["eng"]]
+        waits[i] = []
+        if o["kind"] != "arr":
+            for d in sorted(o["deps"], key=lambda d: -where[d]):
+                if o["deps"][d] and kn.get(chan[d], 0) < pos[d]:
+                    waits[i].append(d)
+                    marked.add(d)
+                    for c, v in clock[d].items():
+                        if kn.get(c, 0) < v:
+                            kn[c] = v
+            clock[i] = dict(kn)
+        else:
+            clock[i] = {}
+        clock[i][chan[i]] = pos[i]
+    value, run = {}, {}
+    for i in order:
+        if ops[i]["kind"] in COMPUTE and i in marked:
+            run[chan[i]] = run.get(chan[i], 0) + 1
+            value[i] = ("c" + chan[i], run[chan[i]])
+        elif ops[i]["kind"] in ("load", "store"):
+            value[i] = (chan[i], 16)
+        elif ops[i]["kind"] == "arr":
+            value[i] = (chan[i], 2 * len(others) * unit)
+
+    Q = {"V": g.vector, "S": g.scalar, "P": g.tensor, "G": g, "Y": g.sync}
+
+    def ap(x):
+        return T[x[0]][x[1]] if isinstance(x, tuple) else x
+
+    total = 0
+    for i in order:
+        o = ops[i]
+        k, a = o["kind"], o["args"]
+        if k == "arr":
+            continue
+        q = Q[o["eng"]]
+        for d in waits[i]:
+            q.wait_ge(T.sem[value[d][0]], value[d][1])
+        if k == "send":
+            tab, lo, hi, via, sem = a
+            total += spread(g, T, topo, core, [helper[core]] if via else others, T[tab][:, lo:hi], T.sem[sem])
+            continue
+        if k == "ts":
+            ins = (q.tensor_scalar(ap(a[0]), ap(a[1]), ap(a[2]), None, a[4]) if a[5] is None
+                   else q.tensor_scalar(ap(a[0]), ap(a[1]), ap(a[2]), ap(a[3]), a[4], a[5]))
+        elif k == "tt":
+            ins = q.tensor_tensor(ap(a[0]), ap(a[1]), ap(a[2]), a[3])
+        elif k == "cp":
+            ins = q.tensor_copy(ap(a[0]), ap(a[1]))
+        elif k == "ms":
+            ins = q.memset(ap(a[0]), a[1])
+        elif k == "scan":
+            ins = q.tensor_tensor_scan(ap(a[0]), ap(a[1]), ap(a[2]), 0.0, ALU.mult, ALU.add)
+        elif k == "act":
+            ins = q.activation(ap(a[0]), ap(a[1]), a[2], bias=ap(a[3]), scale=ap(a[4]))
+        elif k == "gat":
+            src = ap(a[1]).indirect(ap(a[2]))
+            ins = q.tensor_copy(ap(a[0]), src) if o["eng"] == "V" else q.activation(ap(a[0]), src, ACT.Copy)
+        elif k == "mm":
+            ins = q.matmul(ap(a[0]), ap(a[1]), ap(a[2]), a[3], a[4])
+        elif k == "iota":
+            ins = (q.iota(ap(a[0]), a[1], a[2], a[3], allow_small_or_imprecise_dtypes=True) if a[4]
+                   else q.iota(ap(a[0]), a[1], a[2], a[3]))
+        elif k == "sel":
+            ins = q.affine_select(ap(a[0]), ap(a[1]), a[2], a[3], a[4], 0, 1)
+        elif k == "load":
+            ins = q.dma_start(ap(a[0]), T[a[1]][:, a[2]:a[3]])
+        else:
+            ins = q.dma_start(T[a[1]][:, a[2]:a[3]], ap(a[0]))
+        if i in value:
+            ins.then_inc(T.sem[value[i][0]], value[i][1] if k in ("load", "store") else 1)
+    for i in order:
+        if ops[i]["kind"] == "store":
+            g.sync.wait_ge(T.sem[value[i][0]], 16)
+    g.wait_ge(T.sem.sent, total)

@@ -3,37 +3,48 @@ from concourse.mybir import AluOpType as ALU, ActivationFunctionType as ACT
 
 NV = 256
 SEQ = 2048
-SCAN = (1, 3)
-JENG = ("SSSS", "VVSS", "SSSS", "SSSS")
+NCORES = 128
+CFG = {
+    "scan": ((1, 3),) * 6,
+    "jump": ("SSSS", "VVSS", "SSSS", "SSSS"),
+    "jat": (0, 1),
+    "tile": (256, 256, 256, 256, 256, 128),
+    "r": "S", "nl": "V", "dk": "S",
+    "gx": ("GX", "GX", "GJ", "GK", "GX", "GJ"),
+    "ad": ("B6", "B2"), "jb": "B6",
+}
 
 F, BF, H, I32, U16 = "float32", "bfloat16", "float16", "int32", "uint16"
 IDN = {"one": 1.0, "p256": 256.0, "m3": -3.0, "p4": 4.0, "m1": -1.0, "p2": 2.0, "p3": 3.0, "p128": 128.0,
-       "m16": -16.0, "h0": 1792.0, "q0": -3840.0, "h1": -2304.0, "q1": 4352.0, "p32": 32.0, "m128": -128.0}
+       "m16": -16.0, "h0": 1792.0, "q0": -3840.0, "h1": -2304.0, "q1": 4352.0}
 IDK = list(IDN)
+MAGIC = 12582912.0
 SCRATCH = {
     "XT": ("sbuf", [128, 7 * SEQ + NV], BF), "UT": ("sbuf", [128, 7 * SEQ + NV], F),
     "AX": ("sbuf", [128, 4096], BF),
     "GX": ("sbuf", [128, 4096], BF), "GU": ("sbuf", [128, 4096], F), "GJ": ("sbuf", [128, 4096], BF),
-    "GK": ("sbuf", [128, 4096], BF), "PM": ("sbuf", [128, 512], F),
+    "GK": ("sbuf", [128, 4096], BF),
     "PX": ("sbuf", [128, 2048], H), "PU": ("sbuf", [128, 2048], F), "PS": ("sbuf", [128, 1024], F),
-    "MN": ("sbuf", [128, 1536], BF), "SD": ("sbuf", [128, 2048], BF),
+    "MN": ("sbuf", [128, 2048], BF), "SD": ("sbuf", [128, 2048], BF),
     "S0": ("sbuf", [128, 512], I32), "P0": ("sbuf", [128, 512], I32), "AG": ("sbuf", [128, 512], BF),
     "TH": ("sbuf", [128, 4], I32), "QB": ("sbuf", [128, 8], F),
-    "WW": ("sbuf", [128, 2048], BF), "R4": ("sbuf", [128, 2048], BF), "NL": ("sbuf", [128, 1536 + 512], BF),
+    "WW": ("sbuf", [128, 2048], BF), "RR": ("sbuf", [128, 2048], BF), "NL": ("sbuf", [128, 2048], BF),
     "LV": ("sbuf", [128, 512], BF), "WT": ("sbuf", [128, 1536], BF),
-    "CC": ("sbuf", [128, 2048], F), "GG": ("sbuf", [128, 1536], F), "D0": ("sbuf", [128, 512], F),
+    "CC": ("sbuf", [128, 1536], H), "CF": ("sbuf", [128, 1024], F), "GG": ("sbuf", [128, 1536], F),
+    "D0": ("sbuf", [128, 512], F),
     "DG": ("sbuf", [128, 512], F), "TT": ("sbuf", [128, 512], F), "N1": ("sbuf", [128, 512], F),
-    "TA": ("sbuf", [128, 256], F), "TB": ("sbuf", [128, 256], F),
-    "OF": ("sbuf", [128, 24, 64], U16), "OJ": ("sbuf", [128, 1024], U16),
-    "XP": ("sbuf", [128, 256], BF), "HQ": ("sbuf", [128, 512], BF),
+    "TA": ("sbuf", [128, 256], F), "TB": ("sbuf", [128, 256], F), "TC": ("sbuf", [128, 256], F),
+    "OF": ("sbuf", [128, 1536], U16), "OJ": ("sbuf", [128, 1024], U16),
+    "HQ": ("sbuf", [128, 512], BF),
     "KEY": ("sbuf", [128, 256], BF), "FR": ("sbuf", [128, 256], BF), "CAP": ("sbuf", [128, 256], BF),
     "STR": ("sbuf", [128, 256], BF), "OX": ("sbuf", [128, 256], F), "OW": ("sbuf", [128, 256], F),
     "pI": ("sbuf", [128, 8], I32), "COL": ("sbuf", [128, 8], F), "rowm": ("sbuf", [128, 160], F),
     "rowh": ("sbuf", [128, 128], F), "rowl": ("sbuf", [128, 128], F),
-    "ONE": ("sbuf", [128, 256], BF), "SEG": ("sbuf", [128, 512], F), "YY": ("sbuf", [128, 8, 32], BF),
-    "ID": ("sbuf", [128, 128 * len(IDK)], BF), "IH": ("sbuf", [128, 128], H), "IF": ("sbuf", [128, 256], F),
+    "ONE": ("sbuf", [128, 256], BF), "CST": ("sbuf", [128, 256], BF), "SEG": ("sbuf", [128, 512], F),
+    "YY": ("sbuf", [128, 8, 32], BF),
+    "ID": ("sbuf", [128, 128 * len(IDK)], BF), "IH": ("sbuf", [128, 256], H), "IF": ("sbuf", [128, 256], F),
     "KD": ("sbuf", [128, 128], BF), "BO": ("sbuf", [128, 128], BF), "ZZ": ("sbuf", [128, 144], BF),
-    "NM": ("sbuf", [128, 128], BF), "LM": ("sbuf", [128, 128], BF), "KM": ("sbuf", [128, 256], BF),
+    "NM": ("sbuf", [128, 128], BF), "LM": ("sbuf", [128, 128], BF), "KM": ("sbuf", [128, 512], BF),
     "MK": ("sbuf", [128, 32], F), "THR": ("sbuf", [128, 16], F),
     "SW": ("sbuf", [128, 2048], BF), "DK": ("sbuf", [128, 2048], BF), "AD": ("sbuf", [128, 2048], BF),
 }
@@ -43,11 +54,10 @@ NDMA = 20
 SEMAPHORES = (["cV", "cS", "cP", "cG", "sent"] + ["ax%d" % j for j in range(6)] + ["au%d" % j for j in range(6)]
               + ["d%d" % j for j in range(NDMA)])
 
-CY, PC, GR, HOP = 0.00083, 0.00045, 1.5, 0.1
-ROUNDS, SEED, SHAKE = 15, 3, 0.3
-GXB = ("GX", "GX", "GJ", "GK", "GX", "GJ")
+CY, PC, GR, HOP = 0.00083, 0.00043, 1.56, 0.1
+ROUNDS, SEED, SHAKE = 100, 1, 0.3
 ORDER = []
-LAT = {"xa": 7.5, "xb": 4.8, "ua": 9.0, "ub": 6.3, "x0": 14.0, "u0": 20.0}
+LAT = {"xa": 9.0, "xb": 6.5, "ua": 11.0, "ub": 8.5, "x0": 12.0, "u0": 18.0}
 
 
 def span(shape, idx):
@@ -95,7 +105,6 @@ def build(rank):
             where, lo, hi, n, dt = info(x)
             if where == "psum":
                 wr = any(y[0] == x[0] for y in writes)
-                rd = any(y[0] == x[0] for y in reads)
                 if x[0] in seen:
                     continue
                 seen.add(x[0])
@@ -211,23 +220,19 @@ def build(rank):
 
     pc, kc, gc = A("COL", 0, 1), A("COL", 1, 2), A("COL", 2, 3)
     ms(A("ONE"), 1.0)
+    ms(A("CST", 0, 128), -255.0 / 512)
+    ms(A("CST", 128, 256), MAGIC)
     ts(A("pI", 1, 2), A("pI", 0, 1), 15, None, ALU.bitwise_and)
     ts(A("pI", 2, 3), A("pI", 0, 1), 112, None, ALU.bitwise_and)
     cp(A("COL", 0, 3), A("pI", 0, 3))
     ts(idn("one"), A("rowm", 0, 128), pc, None, ALU.is_equal)
-    ts(A("COL", 3, 4), pc, 8.0, None, ALU.add)
-    ts(A("COL", 4, 5), pc, -8.0, None, ALU.add)
-    ts(A("COL", 5, 6), kc, 8.0, None, ALU.is_lt)
-    ts(A("COL", 6, 7), kc, 8.0, None, ALU.is_ge)
-    for j, c in enumerate((0, 3, 4, 0)):
-        ts(A("PM", 128 * j, 128 * j + 128), A("rowm", 0, 128), A("COL", c, c + 1), A("COL", 5 + j // 2, 6 + j // 2),
-           ALU.is_equal, ALU.mult)
     for k in IDK[1:]:
         ts(idn(k), idn("one"), IDN[k], None, ALU.mult)
-    ts(A("IH"), idn("one"), 1.0 / 256, None, ALU.mult)
-    ts(A("IF", 0, 128), idn("one"), 1.0, None, ALU.mult)
-    ts(A("IF", 128, 256), idn("one"), 1024.0, None, ALU.mult)
-    ts(A("KD"), idn("one"), kc, None, ALU.mult)
+    ts(A("IH", 0, 128), idn("one"), 1.0 / 256, None, ALU.mult)
+    ts(A("IH", 128, 256), idn("one"), 1.0, None, ALU.mult)
+    act(A("IF", 0, 128), idn("one"), ACT.Identity)
+    act(A("IF", 128, 256), idn("one"), ACT.Identity, 0.0, 1024.0)
+    act(A("KD"), idn("one"), ACT.Identity, 0.0, kc)
     ts(A("BO"), A("rowh"), gc, None, ALU.is_equal)
     ts(A("ZZ"), A("rowm", 0, 144), -15.0, gc, ALU.add, ALU.is_equal)
     ts(A("MK", 0, 16), A("rowm", 0, 16), kc, None, ALU.is_equal)
@@ -235,19 +240,22 @@ def build(rank):
     for k in range(16):
         ts(A("SW", 128 * k, 128 * k + 128), A("BO"), A("MK", k, k + 1), None, ALU.mult)
     for k in range(16):
-        act(A("DK", 128 * k, 128 * k + 128), idn("one"), ACT.Identity, 0.0, A("MK", 16 + k, 17 + k))
+        if CFG["dk"] == "S":
+            act(A("DK", 128 * k, 128 * k + 128), idn("one"), ACT.Identity, 0.0, A("MK", 16 + k, 17 + k))
+        else:
+            ts(A("DK", 128 * k, 128 * k + 128), idn("one"), A("MK", 16 + k, 17 + k), None, ALU.mult)
     ts(A("KM", 0, 128), A("rowl"), kc, None, ALU.is_equal)
-    tt(A("NM"), A("KM", 0, 128), idn("p32"), ALU.add)
-    ts(A("KM", 128, 256), A("BO"), 2.0, None, ALU.mult)
-    tt(A("LM"), A("KM", 128, 256), idn("m128"), ALU.add)
+    act(A("KM", 128, 256), idn("one"), ACT.Identity, 0.0, 32.0)
+    tt(A("NM"), A("KM", 0, 128), A("KM", 128, 256), ALU.add)
+    act(A("KM", 256, 384), A("BO"), ACT.Identity, 0.0, 2.0)
+    tt(A("LM"), A("KM", 256, 384), idn("p128"), ALU.subtract)
     ts(A("THR", 8, 16), A("rowm", 1, 9), kc, 16.0, ALU.add, ALU.is_ge)
     ts(A("THR", 0, 8), A("THR", 8, 16), -0.5, None, ALU.add)
     cp(A("QB", 0, 2), A("TH", 0, 2))
     ts(A("QB", 2, 3), A("QB", 0, 1), 16.0, None, ALU.add)
     ts(A("QB", 3, 4), A("QB", 1, 2), -1.0, 0.5, ALU.mult, ALU.add)
-    if SCAN:
-        ms(A("SEG"), 1.0)
-        ms(A("SEG", 0, 512, 8), 0.0)
+    ms(A("SEG"), 1.0)
+    ms(A("SEG", 0, 512, 8), 0.0)
     yall = A3("YY", 0, 8, 0, 32)
     j = add("G", "sel", (yall, A("ONE"), [[-16, 8], [0, 2], [-1, 16]], ALU.is_equal, 0.0), [A("ONE")], [yall], 0.6)
     ops[j]["deps"][hist["G", True]] = False
@@ -258,52 +266,45 @@ def build(rank):
     def ad(d):
         return A("AD", 128 * d, 128 * d + 128)
 
-    def columns(stage, b):
+    def columns(stage, b, p):
         c = st("CC", stage, b)
-        act(A("HQ", 0, 256), c, ACT.Identity, 191.501953125, 1.0 / 256)
-        act(A("HQ", 256, 512), c, ACT.Identity, 191.5009765625, 1.0 / 512)
-        p = A("B4", 256, 512)
-        lin(p, [(idn("h%d" % b), A("HQ", 0, 256)), (idn("q%d" % b), A("HQ", 256, 512))])
-        tt(A("TB"), p, c, ALU.add)
-        j = 8 * stage + 4 * b
-        for hk in range(2):
-            lin(A("B4", 256 + 128 * hk, 384 + 128 * hk),
-                [(A("PM", 256 * hk + 128 * h, 256 * hk + 128 * h + 128), A("TB", h, 256, 2)) for h in range(2)])
-        for hk in range(2):
-            ts(A3("OF", j, j + 4, 32 * hk, 32 * hk + 32), A("B4", 256 + 128 * hk, 384 + 128 * hk),
-               393216.0 if b == 0 else 2048.0 - 393216.0, None, ALU.add)
+        ts(A("HQ", 0, 256), c, 1.0 / 256, 199.501953125, ALU.mult, ALU.add)
+        ts(A("HQ", 256, 512), c, 1.0 / 512, 195.5009765625, ALU.mult, ALU.add)
+        lin(p, [(A("IH", 128, 256), c), (idn("h%d" % b), A("HQ", 0, 256)), (idn("q%d" % b), A("HQ", 256, 512))])
+        ts(st("OF", stage, b), p, 2048.0 + 393216.0 if b == 0 else 4096.0 - 393216.0, None, ALU.add)
 
-    def weights(stage, b):
-        p = A("B7", 256, 512)
-        lin(p, [(idn("one"), st("R4", stage, b)), (idn("p3"), st("NL", stage, b))])
+    def weights(stage, b, p):
+        lin(p, [(idn("one"), A("ONE")), (idn("one"), st("RR", stage, b)), (idn("p3"), st("NL", stage, b))])
         tt(st("WT", stage, b), p, st("WW", stage, b), ALU.mult)
 
-    def start(b):
-        ag = st("AG", 0, b)
-        ts(st("LV", 0, b), ag, 3.0, None, ALU.is_lt)
-        p = A("B7", 0, 256)
-        tt(p, st("P0", 0, b), st("S0", 0, b), ALU.subtract)
-        tt(p, p, st("LV", 0, b), ALU.mult)
-        tt(st("CC", 0, b), p, st("S0", 0, b), ALU.add)
-        act(st("TT", 0, b), p, ACT.Identity)
-        cp(st("OJ", 0, b), st("CC", 0, b))
-        columns(0, b)
-        ts(st("NL", 0, b), ag, 3.0, None, ALU.is_equal)
-        ts(st("R4", 0, b), ag, -1.0, 4.0, ALU.mult, ALU.add)
-        weights(0, b)
+    def start():
+        ts(A("LV"), A("AG"), 3.0, None, ALU.is_lt)
+        p = A("B7")
+        tt(p, A("P0"), A("S0"), ALU.subtract)
+        tt(p, p, A("LV"), ALU.mult)
+        tt(A("CF", 0, 512), p, A("S0"), ALU.add)
+        act(A("TT"), p, ACT.Identity)
+        cp(A("OJ", 0, 512), A("CF", 0, 512))
+        ts(A("CC", 0, 512), A("CF", 0, 512), -2048.0, None, ALU.add)
+        ts(A("NL", 0, 512), A("AG"), 3.0, None, ALU.is_equal)
+        ts(A("RR", 0, 512), A("AG"), -1.0, 3.0, ALU.mult, ALU.add)
+        for b in range(2):
+            columns(0, b, A("B4", 0, 256))
+            weights(0, b, A("B5", 0, 256))
 
     def jump(rnd, b):
-        n = st("CC", 0, b) if rnd == 0 else st("N1", 0, b)
+        n = st("CF", 0, b) if rnd == 0 else st("N1", 0, b)
         gj = "GJ" if b == 0 else "GK"
         for ch in range(4):
-            gat(JENG[2 * rnd + b][ch], A(gj, 1024 * ch, 1024 * ch + 1024), A("AX"), st("OJ", rnd, b, 64 * ch, 64 * ch + 64))
-        p = A("B6", 0, 256)
+            gat(CFG["jump"][2 * rnd + b][ch], A(gj, 1024 * ch, 1024 * ch + 1024), A("AX"),
+                st("OJ", rnd, b, 64 * ch, 64 * ch + 64))
+        p = A(CFG["jb"], 0, 256)
         lin(p, [(A("KD"), A("ONE"))] + [(A("DK", 128 * k, 128 * k + 128), A(gj, k, 4096, 16)) for k in range(16)])
-        tt(A("TA"), p, n, ALU.add)
-        ts(A("TB"), A("TA"), 4096.0, -4096.0, ALU.is_ge, ALU.mult)
+        tt(A("TC"), p, n, ALU.add)
+        ts(A("TB"), A("TC"), 4096.0, -4096.0, ALU.is_ge, ALU.mult)
         if rnd == 0:
             tt(st("GG", 0, b), p, A("TB"), ALU.add)
-            q = A("B6", 256, 512)
+            q = A(CFG["jb"], 256, 512)
             mm(q, idn("one"), st("NL", 0, b))
             tt(q, q, st("GG", 0, b), ALU.mult)
             tt(st("N1", 0, b), q, st("S0", 0, b), ALU.add)
@@ -319,28 +320,29 @@ def build(rank):
         b, s = t % 2, t // 2
         for ch in range(4):
             v = 64 * ch
-            gat("S", A(gbuf, 16 * v, 16 * v + 1024), A(tab, t * SEQ, t * SEQ + 2 * SEQ),
-                ("OF", (slice(None), 8 * s + 4 * b + ch)), first)
+            gat("S", A(gbuf, 16 * v, 16 * v + 1024), A(tab, t * SEQ, t * SEQ + 2 * SEQ), st("OF", s, b, v, v + 64), first)
             for hk in range(2):
                 bank = "B%d" % (ring[0] % 2)
                 ring[0] += 1
                 for kk in range(8):
-                    k = 8 * hk + kk
+                    k = 2 * kk + hk
                     mm(A(bank, kk, 512, 8), A("SW", 128 * k, 128 * k + 128), st("WT", s, b, v, v + 64))
                 o = 512 * ((2 * ch + hk) % 4)
-                tt(A(pbuf, o, o + 512), A(gbuf, 16 * v + 512 * hk, 16 * v + 512 * hk + 512), A(bank), ALU.mult)
+                tt(A(pbuf, o, o + 512), A(gbuf, 16 * v + hk, 16 * v + 1024, 2), A(bank), ALU.mult)
                 yield ch, hk, o
 
     def xphase(t):
         sends = []
-        for ch, hk, o in products(t, "XT", GXB[t], "PX", [arrx[t]] if t in arrx else []):
+        for ch, hk, o in products(t, "XT", CFG["gx"][t], "PX", [arrx[t]] if t in arrx else []):
             v = 64 * ch
+            if hk == 0 and ch % 2 == 0:
+                mm(A("B3", v, v + 128), idn("one"), A("CST", 0, 128), True, False)
             for kk in range(8):
-                mm(A("B3", v, v + 64), A("IH"), A("PX", o + kk, o + 512, 8), hk == 0 and kk == 0, hk == 1 and kk == 7)
+                mm(A("B3", v, v + 64), A("IH", 0, 128), A("PX", o + kk, o + 512, 8), False, False)
             if hk == 1 and ch % 2 == 1:
                 a = v - 64
-                ts(A("XP", a, a + 128), A("B3", a, a + 128), 15.0, 191.501953125, ALU.min, ALU.add)
-                ts(A("XT", *own(t + 2, a, a + 128)), A("XP", a, a + 128), -192.0, None, ALU.add)
+                mm(A("B3", a, a + 128), idn("one"), A("CST", 128, 256), False, True)
+                ts(A("XT", *own(t + 2, a, a + 128)), A("B3", a, a + 128), -MAGIC, 15.0, ALU.add, ALU.min)
                 if t < 5:
                     sends.append(send("XT", t + 2, a, a + 128, a == 0, "ax%d" % (t + 1), LAT["xa" if a == 0 else "xb"]))
         if t < 5:
@@ -354,19 +356,19 @@ def build(rank):
 
     def overlap(t):
         b, s = t % 2, t // 2
-        for ch in range(4):
-            a = 64 * ch
-            bank = "B2" if ch % 2 == 0 else "B6"
-            for kk in range(8):
-                mm(A(bank, kk, 512, 8), idn("one"), A("XT", *own(t, a, a + 64)))
-            mm(A("B5", a, a + 64), idn("p256"), st("NL", s, b, a, a + 64), True, False)
-            for hk in range(2):
-                o = 512 * (ring[1] % 3)
+        nv = CFG["tile"][t]
+        m = 512 // nv
+        for a in range(0, NV, nv):
+            for j in range(m):
+                mm(A("B2", j, 512, m), idn("one"), A("XT", *own(t, a, a + nv)))
+            mm(A("B5", a, a + nv), idn("p256"), st("NL", s, b, a, a + nv), True, False)
+            for kk in range(16 // m):
+                o = 512 * (ring[1] % 4)
                 ring[1] += 1
-                tt(A("MN", o, o + 512), A(GXB[t], 16 * a + 512 * hk, 16 * a + 512 * hk + 512), A(bank), ALU.min)
-                for kk in range(8):
-                    k = 8 * hk + kk
-                    mm(A("B5", a, a + 64), A("ZZ", 15 - k, 143 - k), A("MN", o + kk, o + 512, 8), False, k == 15)
+                tt(A("MN", o, o + 512), A(CFG["gx"][t], 16 * a + kk, 16 * (a + nv), 16 // m), A("B2"), ALU.min)
+                for j in range(m):
+                    k = kk + 16 // m * j
+                    mm(A("B5", a, a + nv), A("ZZ", 15 - k, 143 - k), A("MN", o + j, o + 512, m), False, k == 15)
         act(A("KEY"), A("B5", 0, 256), ACT.Identity, -240.0)
         ts(A("FR"), A("KEY"), A("QB", 2, 3), None, ALU.is_ge)
 
@@ -379,7 +381,7 @@ def build(rank):
             if hk == 0:
                 mm(r, idn("p128"), A("XT", *own(t, v, v + 64)), True, False)
                 mm(r, A("IF", 128, 256), A("UT", *own(t, v, v + 64)), False, False)
-            if ch in SCAN:
+            if ch in CFG["scan"][t]:
                 scan(A("PS", 512 * hk, 512 * hk + 512), A("SEG"), A("PU", o, o + 512))
                 mm(r, A("IF", 0, 128), A("PS", 512 * hk + 7, 512 * hk + 512, 8), False, hk == 1)
             else:
@@ -400,60 +402,70 @@ def build(rank):
         b, s = t % 2, t // 2
         nl, nn = st("NL", s, b), st("NL", s + 1, b)
         for j in range(4):
-            bank = "B6" if j % 2 == 0 else "B2"
+            bank = CFG["ad"][j % 2]
             for e in range(2):
                 mm(A(bank, 256 * e, 256 * e + 256), ad(2 * j + e + 1), A("KEY"))
             for e in range(2):
                 d = 2 * j + e
                 act(A("SD", 256 * d, 256 * d + 256), A(bank, 256 * e, 256 * e + 256), ACT.Sign, A("THR", d, d + 1))
-        z = A("B5", 256, 512)
+        z = A("B7", 0, 256)
         lin(z, [(A("LM"), nl), (A("NM"), A("STR"))]
             + [(ad(15 - d) if d < 7 else idn("m1"), A("SD", 256 * d, 256 * d + 256)) for d in range(8)])
         ts(A("CAP"), z, 40.0, None, ALU.is_gt)
-        p, q = A("B7", 0, 256), A("B7", 256, 512)
-        lin(p, [(idn("one"), st("R4", s, b)), (idn("p4"), A("FR")), (idn("m3"), A("CAP"))])
+        p, q = A("B6", 0, 256), A("B7", 256, 512)
+        rn = st("RR", s + 1, b)
+        lin(p, [(idn("one"), st("RR", s, b)), (idn("p4"), A("FR")), (idn("m3"), A("CAP"))])
         lin(q, [(idn("one"), st("WW", s, b)), (idn("p4"), A("CAP"))])
-        ts(st("R4", s + 1, b), p, -1.0, 1.0, ALU.add, ALU.max)
+        if CFG["r"] == "S":
+            act(rn, p, ACT.Relu, -1.0)
+        else:
+            ts(rn, p, -1.0, 0.0, ALU.add, ALU.max)
         ts(st("WW", s + 1, b), q, 15.0, None, ALU.min)
-        ts(nn, st("R4", s + 1, b), 1.0, None, ALU.is_equal)
-        c, cn, d0 = st("CC", s, b), st("CC", s + 1, b), st("D0", 0, b)
+        if CFG["nl"] == "S":
+            act(nn, rn, ACT.Relu, 1.0, -1.0)
+        else:
+            ts(nn, rn, 0.0, None, ALU.is_equal)
+        d0 = st("D0", 0, b)
+        c, cn = (st("CC", s, b), st("CC", s + 1, b)) if s < 2 else (st("CF", 1, b), st("CF", 0, b))
 
         def ended(out, f):
             lin(out, [(idn("m1"), nl), (idn(f), A("FR")), (idn("m1"), A("CAP")), (idn("one"), nn)])
-        u, w = A("B5", 0, 256), A("B5", 256, 512)
+        p, u, w = A("B7", 0, 256), A("B6", 0, 256), A("B6", 256, 512)
         if s == 0:
             ended(u, "p2")
             tt(w, u, d0, ALU.mult)
             tt(cn, w, c, ALU.add)
         else:
             mm(p, idn("one"), A("FR"))
+            tt(p, p, st("GG", s, b), ALU.mult)
+            tt(A("TA"), p, c, ALU.add)
             ended(w, "one")
             if s == 1:
                 ended(u, "p2")
-            tt(p, p, st("GG", s, b), ALU.mult)
-            tt(A("TA"), p, c, ALU.add)
             tt(w, w, d0, ALU.mult)
             tt(cn, w, A("TA"), ALU.add)
         if s < 2:
-            columns(s + 1, b)
-            weights(s + 1, b)
+            weights(s + 1, b, A("B7", 0, 256))
+            columns(s + 1, b, A("B7", 256, 512))
             tt(u, u, st("DG", 0, b), ALU.mult)
             tt(st("GG", s + 1, b), u, st("GG", s, b), ALU.add)
+            if s == 1:
+                ts(st("CF", 1, b), cn, 2048.0, None, ALU.add)
         else:
             store("yc", b * NV, b * NV + NV, cn)
-            lin(p, [(idn("m16"), st("R4", 3, b)), (idn("one"), st("WW", 3, b))])
-            act(A("OW"), p, ACT.Identity, 64.0)
+            lin(p, [(idn("m16"), rn), (idn("one"), st("WW", 3, b))])
+            act(A("OW"), p, ACT.Identity, 48.0)
             store("yw", b * NV, b * NV + NV, A("OW"))
 
-    start(0)
-    start(1)
+    start()
     jump(0, 0)
     jump(0, 1)
     for t in range(6):
         xphase(t)
         overlap(t)
-        if t < 2:
-            jump(1, t)
+        for b in range(2):
+            if CFG["jat"][b] == t:
+                jump(1, b)
         uphase(t)
         update(t)
     return ops
@@ -513,53 +525,71 @@ COMPUTE = ("ts", "tt", "cp", "ms", "scan", "act", "gat", "mm", "iota", "sel")
 
 
 def routes(T, topo):
-    helper = {}
+    chips = sorted(set(topo.chip(c) for c in T.cores))
+    ranks = dict((x, [c for c in T.cores if topo.chip(c) == x]) for x in chips)
+    out, land = {}, dict(((c, via), []) for c in T.cores for via in (True, False))
     for c in T.cores:
-        for h in topo.cores_of(c):
-            if (h not in T.cores and h not in helper.values() and topo.die(h) != topo.die(c)
-                    and all(topo.may_write(h, d) for d in T.cores)):
-                helper[c] = h
-                break
-    return helper
+        out[c] = [h for h in topo.cores_of(c) if h not in T.cores and h not in out.values()
+                  and topo.die(h) != topo.die(c) and all(topo.may_write(h, d) for d in T.cores)][0]
+    for x in chips:
+        plane = [y for y in chips if y == x or topo.same_plane(x, y)]
+        round_mate = [y for y in chips if y not in plane][plane.index(x)]
+        near = [h for h in topo.cores_of(ranks[x][0]) if h not in T.cores and h not in out.values()]
+        mate = [h for h in range(NCORES) if topo.mates(topo.chip(h), x) and topo.may_write(h, ranks[x][0])]
+        for j, c in enumerate([c for c in T.cores if topo.chip(c) not in (x, round_mate)]):
+            land[c, True].append(near[j])
+            land[c, False].append(near[j])
+        for j, c in enumerate(ranks[round_mate]):
+            for via in (True, False):
+                land[c, via].append([h for h in mate if topo.die(h) == topo.die(out[c] if via else c)][j])
+    return out, land
 
 
-def spread(g, T, topo, src, dsts, ap, sem):
-    far = [d for d in dsts if topo.chip(d) != topo.chip(src)]
-    near = [d for d in dsts if d not in far]
-    outer = topo.mask(src, [c for c in T.cores if topo.chip(c) != topo.chip(src)][0])
-    tr = []
-    for ds in (far, near):
-        if ds:
-            m = outer if ds is far else topo.mask(src, ds[0]) & ~outer
-            tr.append(RemoteDMATransfer(dst_ids=[DstId(rid=topo.addr(d)[0], pnc=topo.addr(d)[1]) for d in ds],
-                                        dma_engine_mask=m, remote_sem=sem, srcs=[ap], dsts=[ap] * len(ds)))
-    g.remote_dma_fused(tr, local_sem=T.sem.sent)
-    return sum(bin(t_m).count("1") for t_m in ([outer] if far else []) + ([topo.mask(src, near[0]) & ~outer] if near else []))
+def fused(g, T, topo, parts):
+    g.remote_dma_fused([RemoteDMATransfer(dst_ids=[DstId(rid=topo.addr(d)[0], pnc=topo.addr(d)[1]) for d in ds],
+                                          dma_engine_mask=sum(1 << e for e in es), remote_sem=sem, srcs=[ap],
+                                          dsts=[ap] * len(ds)) for ds, es, ap, sem in parts], local_sem=T.sem.sent)
+    return sum(len(p[1]) for p in parts)
 
 
 def rank_program(g, core, T, topo):
-    helper = routes(T, topo)
-    rank = T.rank_of(core)
-    owner = [c for c in helper if helper[c] == core]
-    if rank is None and not owner:
+    out, land = routes(T, topo)
+    owner = [c for c in T.cores if core in [c, out[c]] + land[c, True] + land[c, False]]
+    if not owner:
         return
-    me = core if rank is not None else owner[0]
-    others = [c for c in T.cores if c != me]
+    me = owner[0]
+    sib = [c for c in T.cores if c != me and topo.chip(c) == topo.chip(me)][0]
     ops = build(T.rank_of(me))
     if not ORDER:
         ORDER.extend(schedule(ops))
     order = ORDER
-    far1 = [c for c in T.cores if topo.chip(c) != topo.chip(me)][0]
-    unit = len(topo.engines(me, far1))
-    if rank is None:
-        total = 0
-        for i in order:
-            if ops[i]["kind"] == "send" and ops[i]["args"][3]:
-                tab, lo, hi, via, sem = ops[i]["args"]
-                g.wait_ge(T.sem[sem], unit)
-                total += spread(g, T, topo, core, others, T[tab][:, lo:hi], T.sem[sem])
+    outer = topo.engines(me, land[me, False][0])
+    inner = [e for e in topo.engines(me, sib) if e not in outer]
+    sends = [ops[i]["args"] for i in order if ops[i]["kind"] == "send"]
+    total = 0
+    if core == out[me]:
+        for tab, lo, hi, via, sem in sends:
+            if via:
+                g.wait_ge(T.sem[sem], len(inner))
+                total += fused(g, T, topo, [(land[me, True], outer, T[tab][:, lo:hi], T.sem[sem])])
+    elif core != me:
+        to = [c for c in T.cores if topo.chip(c) == topo.chip(core) or topo.mates(topo.chip(c), topo.chip(core))]
+        eng = topo.engines(core, to[0])
+        for j in range(0, len(sends), 2):
+            mine = [s for s in sends[j:j + 2] if core in land[me, s[3]]]
+            tab, sem = mine[0][0], T.sem[mine[0][4]]
+            g.wait_ge(sem, len(mine) * len(outer))
+            if mine[0][2] == mine[-1][1]:
+                mine = [(tab, mine[0][1], mine[-1][2])]
+            n = len(eng) // len(mine)
+            total += fused(g, T, topo, [(to, eng[n * e:n * e + n], T[tab][:, s[1]:s[2]], sem) for e, s in enumerate(mine)])
+    if core != me:
         g.wait_ge(T.sem.sent, total)
         return
+    arrivals = len(outer) + len(inner)
+    for h in set(h for c in T.cores for via in (True, False) for h in land[c, via]):
+        if topo.chip(h) == topo.chip(me) or topo.mates(topo.chip(h), topo.chip(me)):
+            arrivals += len(topo.engines(h, me))
 
     pos, cnt, chan = {}, {}, {}
     nd = 0
@@ -601,14 +631,13 @@ def rank_program(g, core, T, topo):
         elif ops[i]["kind"] in ("load", "store"):
             value[i] = (chan[i], 16)
         elif ops[i]["kind"] == "arr":
-            value[i] = (chan[i], 2 * len(others) * unit)
+            value[i] = (chan[i], arrivals)
 
     Q = {"V": g.vector, "S": g.scalar, "P": g.tensor, "G": g, "Y": g.sync}
 
     def ap(x):
         return T[x[0]][x[1]] if isinstance(x, tuple) else x
 
-    total = 0
     for i in order:
         o = ops[i]
         k, a = o["kind"], o["args"]
@@ -619,7 +648,11 @@ def rank_program(g, core, T, topo):
             q.wait_ge(T.sem[value[d][0]], value[d][1])
         if k == "send":
             tab, lo, hi, via, sem = a
-            total += spread(g, T, topo, core, [helper[core]] if via else others, T[tab][:, lo:hi], T.sem[sem])
+            a, s = T[tab][:, lo:hi], T.sem[sem]
+            if via:
+                total += fused(g, T, topo, [([out[me]], inner, a, s), ([sib], outer, a, s)])
+            else:
+                total += fused(g, T, topo, [(land[me, False], outer, a, s), ([sib], inner, a, s)])
             continue
         if k == "ts":
             ins = (q.tensor_scalar(ap(a[0]), ap(a[1]), ap(a[2]), None, a[4]) if a[5] is None

@@ -5,18 +5,28 @@ NV = 256
 SEQ = 2048
 NCORES = 128
 CFG = {
-    "scan": ((1, 3),) * 6,
-    "jump": ("SSSS", "VVSS", "SSSS", "SSSS"),
+    "scan": ("msmsmsms",) * 6,
+    "jump": (("S4",), ("V2", "V1", "S1"), ("S1", "S1", "S1", "V1"), ("S1", "S1", "S1", "V1")),
     "jat": (0, 1),
-    "tile": (256, 256, 256, 256, 256, 128),
-    "r": "S", "nl": "V", "dk": "S",
+    "tile": (128, 128, 128, 128, 128, 128),
+    "r": "S", "nl": "S", "dk": "G" * 8 + "S" * 8, "sw": "V" * 8 + "G" * 8, "ct": True,
+    "late": ("p256", "m3", "p4", "m1", "p2", "m16", "m15", "mh"), "ids": (), "cap": "SSSSSS", "pj": True,
     "gx": ("GX", "GX", "GJ", "GK", "GX", "GJ"),
-    "ad": ("B6", "B2"), "jb": "B6",
+    "ad": ("B6", "B7"), "jb": "B7", "ring": ("B0", "B1"), "rb": (("B4", 0), ("B3", 0)), "cb": ("B5", 0), "kb": ("B5", 256),
+    "XT": ("SSSS",) * 6, "UT": ("SSSS",) * 6, "wb": ("B0", "B1"), "abs": ("VV",) * 6,
+    "eb": ("B3", 256), "seq": "oju", "zb": "B6",
 }
+AT = {"early": 3.0, "T0": 16.0, "P": 16.5, "tile": 0.5, "lead": 0.7, "lag": 0.5,
+      "Xg0": 0.0, "Xg1": 1.4, "Xg2": 5.5, "Xg3": 6.9, "Xp0": 2.3, "Xp1": 3.3, "Xp2": 6.9, "Xp3": 8.3,
+      "Ug0": 8.3, "Ug1": 9.7, "Ug2": 11.1, "Ug3": 12.5, "Up0": 9.7, "Up1": 11.1, "Up2": 12.6, "Up3": 14.0,
+      "th0": 11.1, "th1": 12.5, "th2": 13.9, "th3": 15.8, "str": 14.2, "m0": 4.4, "m1": 5.4, "m2": 15.5, "m3": 16.5,
+      "key": 19.3, "fr": 19.7, "sd0": 19.7, "sd1": 20.3, "sd2": 20.9, "sd3": 21.5, "z": 22.0, "cap": 22.5, "rr": 23.4,
+      "ww": 23.4, "nl": 23.9, "cn": 24.3, "wt": 25.0, "of": 25.3, "gg": 26.0,
+      "j0": 8.0, "j1": 10.0, "j2": 22.0, "j3": 30.0, "jp": 1.4}
 
 F, BF, H, I32, U16 = "float32", "bfloat16", "float16", "int32", "uint16"
 IDN = {"one": 1.0, "p256": 256.0, "m3": -3.0, "p4": 4.0, "m1": -1.0, "p2": 2.0, "p3": 3.0, "p128": 128.0,
-       "m16": -16.0, "h0": 1792.0, "q0": -3840.0, "h1": -2304.0, "q1": 4352.0}
+       "m16": -16.0, "m15": -1.5, "mh": -0.5, "h0": 1792.0, "q0": -3840.0, "h1": -2304.0, "q1": 4352.0}
 IDK = list(IDN)
 MAGIC = 12582912.0
 SCRATCH = {
@@ -32,19 +42,20 @@ SCRATCH = {
     "LV": ("sbuf", [128, 512], BF), "WT": ("sbuf", [128, 1536], BF),
     "CC": ("sbuf", [128, 1536], H), "CF": ("sbuf", [128, 1024], F), "GG": ("sbuf", [128, 1536], F),
     "D0": ("sbuf", [128, 512], F),
-    "DG": ("sbuf", [128, 512], F), "TT": ("sbuf", [128, 512], F), "N1": ("sbuf", [128, 512], F),
-    "TA": ("sbuf", [128, 256], F), "TB": ("sbuf", [128, 256], F), "TC": ("sbuf", [128, 256], F),
+    "DG": ("sbuf", [128, 512], F), "TT": ("sbuf", [128, 512], F), "NC": ("sbuf", [128, 512], H),
+    "TA": ("sbuf", [128, 256], F), "TW": ("sbuf", [128, 256], BF), "JC": ("sbuf", [128, 256], H), "SC": ("sbuf", [128, 512], H),
     "OF": ("sbuf", [128, 1536], U16), "OJ": ("sbuf", [128, 1024], U16),
-    "HQ": ("sbuf", [128, 512], BF),
-    "KEY": ("sbuf", [128, 256], BF), "FR": ("sbuf", [128, 256], BF), "CAP": ("sbuf", [128, 256], BF),
-    "STR": ("sbuf", [128, 256], BF), "OX": ("sbuf", [128, 256], F), "OW": ("sbuf", [128, 256], F),
+    "NB": ("sbuf", [128, 16], BF), "BM": ("sbuf", [128, 128], BF),
+    "HQ": ("sbuf", [128, 512], BF), "CT": ("sbuf", [128, 256], BF),
+    "KEY": ("sbuf", [128, 512], BF), "FR": ("sbuf", [128, 512], BF), "CAP": ("sbuf", [128, 256], BF),
+    "STR": ("sbuf", [128, 512], BF), "NUL": ("sbuf", [128, 128], BF), "I16": ("sbuf", [128, 128], BF), "OX": ("sbuf", [128, 256], F), "OW": ("sbuf", [128, 256], F),
     "pI": ("sbuf", [128, 8], I32), "COL": ("sbuf", [128, 8], F), "rowm": ("sbuf", [128, 160], F),
     "rowh": ("sbuf", [128, 128], F), "rowl": ("sbuf", [128, 128], F),
-    "ONE": ("sbuf", [128, 256], BF), "CST": ("sbuf", [128, 256], BF), "SEG": ("sbuf", [128, 512], F),
+    "ONE": ("sbuf", [128, 256], BF), "CST": ("sbuf", [128, 256], BF), "SEG": ("sbuf", [128, 512], BF),
     "YY": ("sbuf", [128, 8, 32], BF),
-    "ID": ("sbuf", [128, 128 * len(IDK)], BF), "IH": ("sbuf", [128, 256], H), "IF": ("sbuf", [128, 256], F),
+    "ID": ("sbuf", [128, 128 * len(IDK)], BF), "IH": ("sbuf", [128, 384], H), "IF": ("sbuf", [128, 256], F),
     "KD": ("sbuf", [128, 128], BF), "BO": ("sbuf", [128, 128], BF), "ZZ": ("sbuf", [128, 144], BF),
-    "NM": ("sbuf", [128, 128], BF), "LM": ("sbuf", [128, 128], BF), "KM": ("sbuf", [128, 512], BF),
+    "NM": ("sbuf", [128, 128], BF), "LM": ("sbuf", [128, 128], BF), "KM": ("sbuf", [128, 256], BF),
     "MK": ("sbuf", [128, 32], F), "THR": ("sbuf", [128, 16], F),
     "SW": ("sbuf", [128, 2048], BF), "DK": ("sbuf", [128, 2048], BF), "AD": ("sbuf", [128, 2048], BF),
 }
@@ -52,12 +63,14 @@ for _b in range(8):
     SCRATCH["B%d" % _b] = ("psum", [128, 512], F)
 NDMA = 20
 SEMAPHORES = (["cV", "cS", "cP", "cG", "sent"] + ["ax%d" % j for j in range(6)] + ["au%d" % j for j in range(6)]
-              + ["d%d" % j for j in range(NDMA)])
+              + ["bu%d" % j for j in range(1, 6)] + ["d%d" % j for j in range(NDMA)])
 
-CY, PC, GR, HOP = 0.00083, 0.00043, 1.56, 0.1
-ROUNDS, SEED, SHAKE = 100, 1, 0.3
+CY, PC, GR, HOP = 0.00083, 0.00043, 1.56, 0.17
+ROUNDS, SEED, SHAKE, RESTART, AHEAD, URGENT, TIGHT = 16, 3, 0.3, 8, 1.0, 0.5, 0.95
+TRIES = 500
+CASES = ((1, 1, 1), (1, 1.4, 1), (0.72, 1.15, 1), (1.25, 1.2, 1.1))
 ORDER = []
-LAT = {"xa": 9.0, "xb": 6.5, "ua": 11.0, "ub": 8.5, "x0": 12.0, "u0": 18.0}
+LAT = {"xa": 8.3, "xb": 5.8, "ua": 8.7, "ub": 6.7, "x0": 11.5, "u0": 17.0}
 
 
 def span(shape, idx):
@@ -89,6 +102,7 @@ def A3(name, a, b, c, d=None):
 def build(rank):
     ops = []
     hist = {}
+    now = [None]
 
     def info(x):
         where, shape, dt = SCRATCH[x[0]]
@@ -130,7 +144,7 @@ def build(rank):
             if (eng, kind != "load") in hist:
                 deps.setdefault(hist[eng, kind != "load"], False)
             hist[eng, kind != "load"] = i
-        ops.append({"eng": eng, "kind": kind, "args": args, "deps": deps, "cost": cost, "lat": lat})
+        ops.append({"eng": eng, "kind": kind, "args": args, "deps": deps, "cost": cost, "lat": lat, "when": now[0]})
         return i
 
     def isap(x):
@@ -190,9 +204,9 @@ def build(rank):
         o = j * SEQ + (rank * NV if j < 7 else 0)
         return o + a, o + b
 
-    def send(tab, j, a, b, via, sem, lat):
+    def send(tab, j, a, b, via, sem, lat, hop=None):
         lo, hi = own(j, a, b)
-        return add("G", "send", (tab, lo, hi, via, sem), [A(tab, lo, hi)], [], 0.5, lat=lat)
+        return add("G", "send", (tab, lo, hi, via, sem, hop or sem), [A(tab, lo, hi)], [], 0.5, lat=lat)
 
     def arr(sem, sends):
         return add("A", "arr", (sem,), [], [], 0.0, extra=sends)
@@ -226,29 +240,56 @@ def build(rank):
     ts(A("pI", 2, 3), A("pI", 0, 1), 112, None, ALU.bitwise_and)
     cp(A("COL", 0, 3), A("pI", 0, 3))
     ts(idn("one"), A("rowm", 0, 128), pc, None, ALU.is_equal)
+    behind = hist["G", True]
+
+    def sel(out, src, pattern, op, fill, base=0, cm=1):
+        j = add("G", "sel", (out, src, pattern, op, fill, base, cm), [src], [out], 0.17 + 2 * CY * info(out)[3])
+        ops[j]["deps"].setdefault(behind, False)
+
+    if CFG["late"]:
+        ms(A("NUL"), 0.0)
     for k in IDK[1:]:
-        ts(idn(k), idn("one"), IDN[k], None, ALU.mult)
+        if k in CFG["late"]:
+            sel(idn(k), A("NUL"), [[-1, 128]], ALU.not_equal, IDN[k])
+        elif k in CFG["ids"]:
+            act(idn(k), idn("one"), ACT.Identity, 0.0, IDN[k])
+        else:
+            ts(idn(k), idn("one"), IDN[k], None, ALU.mult)
     ts(A("IH", 0, 128), idn("one"), 1.0 / 256, None, ALU.mult)
     ts(A("IH", 128, 256), idn("one"), 1.0, None, ALU.mult)
+    ts(A("IH", 256, 384), idn("one"), -1.0, None, ALU.mult)
     act(A("IF", 0, 128), idn("one"), ACT.Identity)
     act(A("IF", 128, 256), idn("one"), ACT.Identity, 0.0, 1024.0)
     act(A("KD"), idn("one"), ACT.Identity, 0.0, kc)
     ts(A("BO"), A("rowh"), gc, None, ALU.is_equal)
-    ts(A("ZZ"), A("rowm", 0, 144), -15.0, gc, ALU.add, ALU.is_equal)
+    if not CFG["ct"]:
+        ts(A("ZZ"), A("rowm", 0, 144), -15.0, gc, ALU.add, ALU.is_equal)
+    act(A("NB", 0, 8), A("BO", 0, 128, 16), ACT.Identity, 0.0, -1.0)
+    sel(A("BM"), A("BO"), [[0, 32], [1, 4]], ALU.is_equal, 0.0, -3, 0)
     ts(A("MK", 0, 16), A("rowm", 0, 16), kc, None, ALU.is_equal)
     ts(A("MK", 16, 32), A("MK", 0, 16), 16.0, None, ALU.mult)
+    if "G" in CFG["dk"]:
+        act(A("I16"), idn("one"), ACT.Identity, 0.0, 16.0)
     for k in range(16):
-        ts(A("SW", 128 * k, 128 * k + 128), A("BO"), A("MK", k, k + 1), None, ALU.mult)
-    for k in range(16):
-        if CFG["dk"] == "S":
-            act(A("DK", 128 * k, 128 * k + 128), idn("one"), ACT.Identity, 0.0, A("MK", 16 + k, 17 + k))
+        o = A("DK", 128 * k, 128 * k + 128)
+        if CFG["dk"][k] == "S":
+            act(o, idn("one"), ACT.Identity, 0.0, A("MK", 16 + k, 17 + k))
+        elif CFG["dk"][k] == "V":
+            ts(o, idn("one"), A("MK", 16 + k, 17 + k), None, ALU.mult)
         else:
-            ts(A("DK", 128 * k, 128 * k + 128), idn("one"), A("MK", 16 + k, 17 + k), None, ALU.mult)
+            sel(o, A("I16"), [[0, 8], [1, 16]], ALU.is_equal, 0.0, -k, 0)
+    for k in range(16):
+        o = A("SW", 128 * k, 128 * k + 128)
+        if CFG["sw"][k] == "S":
+            act(o, A("BO"), ACT.Identity, 0.0, A("MK", k, k + 1))
+        elif CFG["sw"][k] == "V":
+            ts(o, A("BO"), A("MK", k, k + 1), None, ALU.mult)
+        else:
+            sel(o, A("ONE", 0, 128), [[-16, 8], [0, 16]], ALU.is_equal, 0.0, -k, 1)
     ts(A("KM", 0, 128), A("rowl"), kc, None, ALU.is_equal)
-    act(A("KM", 128, 256), idn("one"), ACT.Identity, 0.0, 32.0)
-    tt(A("NM"), A("KM", 0, 128), A("KM", 128, 256), ALU.add)
-    act(A("KM", 256, 384), A("BO"), ACT.Identity, 0.0, 2.0)
-    tt(A("LM"), A("KM", 256, 384), idn("p128"), ALU.subtract)
+    sel(A("NM"), A("KM", 0, 128), [[-1, 128]], ALU.not_equal, 33.0)
+    act(A("KM", 128, 256), A("BO"), ACT.Identity, 0.0, 2.0)
+    sel(A("LM"), A("KM", 128, 256), [[-1, 128]], ALU.not_equal, -126.0)
     ts(A("THR", 8, 16), A("rowm", 1, 9), kc, 16.0, ALU.add, ALU.is_ge)
     ts(A("THR", 0, 8), A("THR", 8, 16), -0.5, None, ALU.add)
     cp(A("QB", 0, 2), A("TH", 0, 2))
@@ -256,12 +297,13 @@ def build(rank):
     ts(A("QB", 3, 4), A("QB", 1, 2), -1.0, 0.5, ALU.mult, ALU.add)
     ms(A("SEG"), 1.0)
     ms(A("SEG", 0, 512, 8), 0.0)
+    if any(u[ch] == "F" and c[2 * ch] == "s" for u, c in zip(CFG["UT"], CFG["scan"]) for ch in range(4)):
+        ms(A("SEH"), 1.0)
+        ms(A("SEH", 0, 1024, 16), 0.0)
     yall = A3("YY", 0, 8, 0, 32)
-    j = add("G", "sel", (yall, A("ONE"), [[-16, 8], [0, 2], [-1, 16]], ALU.is_equal, 0.0), [A("ONE")], [yall], 0.6)
-    ops[j]["deps"][hist["G", True]] = False
+    sel(yall, A("ONE"), [[-16, 8], [0, 2], [-1, 16]], ALU.is_equal, 0.0)
     for d in list(range(1, 16)):
-        o, y = A("AD", 128 * d, 128 * d + 128), A3("YY", 0, 8, d, d + 16)
-        add("G", "sel", (o, y, [[-1, 128]], ALU.not_equal, -1.0), [y], [o], 0.39)
+        sel(A("AD", 128 * d, 128 * d + 128), A3("YY", 0, 8, d, d + 16), [[-1, 128]], ALU.not_equal, -1.0)
 
     def ad(d):
         return A("AD", 128 * d, 128 * d + 128)
@@ -278,7 +320,9 @@ def build(rank):
         tt(st("WT", stage, b), p, st("WW", stage, b), ALU.mult)
 
     def start():
-        ts(A("LV"), A("AG"), 3.0, None, ALU.is_lt)
+        act(A("NL", 0, 512), A("AG"), ACT.Relu, -2.0)
+        act(A("LV"), A("NL", 0, 512), ACT.Identity, 1.0, -1.0)
+        act(A("RR", 0, 512), A("AG"), ACT.Identity, 3.0, -1.0)
         p = A("B7")
         tt(p, A("P0"), A("S0"), ALU.subtract)
         tt(p, p, A("LV"), ALU.mult)
@@ -286,19 +330,39 @@ def build(rank):
         act(A("TT"), p, ACT.Identity)
         cp(A("OJ", 0, 512), A("CF", 0, 512))
         ts(A("CC", 0, 512), A("CF", 0, 512), -2048.0, None, ALU.add)
-        ts(A("NL", 0, 512), A("AG"), 3.0, None, ALU.is_equal)
-        ts(A("RR", 0, 512), A("AG"), -1.0, 3.0, ALU.mult, ALU.add)
+        if CFG["pj"]:
+            ts(A("SC"), A("S0"), -2048.0, None, ALU.add)
         for b in range(2):
             columns(0, b, A("B4", 0, 256))
             weights(0, b, A("B5", 0, 256))
 
     def jump(rnd, b):
-        n = st("CF", 0, b) if rnd == 0 else st("N1", 0, b)
         gj = "GJ" if b == 0 else "GK"
-        for ch in range(4):
-            gat(CFG["jump"][2 * rnd + b][ch], A(gj, 1024 * ch, 1024 * ch + 1024), A("AX"),
-                st("OJ", rnd, b, 64 * ch, 64 * ch + 64))
+        ch = 0
+        for e, w in CFG["jump"][2 * rnd + b]:
+            now[0] = AT["j%d" % (2 * rnd + b)] + AT["jp"] * ch
+            gat(e, A(gj, 1024 * ch, 1024 * (ch + int(w))), A("AX"), st("OJ", rnd, b, 64 * ch, 64 * (ch + int(w))))
+            ch += int(w)
         p = A(CFG["jb"], 0, 256)
+        if CFG["pj"]:
+            n = st("CC", 0, b) if rnd == 0 else st("NC", 0, b)
+            mm(p, A("KD"), A("ONE"), True, False)
+            mm(p, A("IH", 128, 256), n, False, False)
+            for k in range(16):
+                mm(p, A("DK", 128 * k, 128 * k + 128), A(gj, k, 4096, 16), False, k == 15)
+            ts(A("TW"), p, 2048.0, -4096.0, ALU.is_ge, ALU.mult)
+            tt(A("JC"), p, A("TW"), ALU.add)
+            q, p = p, A(CFG["jb"], 256, 512)
+            lin(p, [(A("IH", 256, 384), n), (A("IH", 128, 256), A("JC"))])
+            if rnd == 0:
+                tt(q, p, st("NL", 0, b), ALU.mult)
+                tt(st("NC", 0, b), q, st("SC", 0, b), ALU.add)
+                ts(st("OJ", 1, b), st("NC", 0, b), 2048.0, None, ALU.add)
+                tt(st("D0", 0, b), q, st("TT", 0, b), ALU.subtract)
+                act(st("GG", 0, b), p, ACT.Identity)
+            else:
+                tt(st("DG", 0, b), p, st("GG", 0, b), ALU.subtract)
+            return
         lin(p, [(A("KD"), A("ONE"))] + [(A("DK", 128 * k, 128 * k + 128), A(gj, k, 4096, 16)) for k in range(16)])
         tt(A("TC"), p, n, ALU.add)
         ts(A("TB"), A("TC"), 4096.0, -4096.0, ALU.is_ge, ALU.mult)
@@ -316,19 +380,42 @@ def build(rank):
 
     ring = [0, 0, 0]
 
+    def at(t, name, plus=0.0):
+        now[0] = AT["T0"] + AT["P"] * t + AT[name] + plus
+
     def products(t, tab, gbuf, pbuf, first):
         b, s = t % 2, t // 2
         for ch in range(4):
             v = 64 * ch
-            gat("S", A(gbuf, 16 * v, 16 * v + 1024), A(tab, t * SEQ, t * SEQ + 2 * SEQ), st("OF", s, b, v, v + 64), first)
+            at(t, tab[0] + "g%d" % ch)
+            who = CFG[tab][t][ch]
+            if who == "F":
+                o = 1024 * (ch % 2)
+                w = A("WS", 1024 * (ch // 2), 1024 * (ch // 2) + 1024)
+                off, win = st("OF", s, b, v, v + 64), A(tab, t * SEQ, t * SEQ + 2 * SEQ)
+                at(t, tab[0] + "p%d" % ch)
+                add("V", "gtt", (A(pbuf, o, o + 1024), win, off, w), [win, off, w], [A(pbuf, o, o + 1024)],
+                    0.06 + 1024 * GR * CY, first)
+                at(t, tab[0] + "p%d" % ch, AT["lag"])
+                yield ch, 2, o
+                continue
+            w = 64 // len(who)
+            go = 1024 * ch
+            for j, e in enumerate(who):
+                a = v + w * j
+                gat(e, A(gbuf, go + 16 * w * j, go + 16 * w * (j + 1)), A(tab, t * SEQ, t * SEQ + 2 * SEQ),
+                    st("OF", s, b, a, a + w), first)
             for hk in range(2):
-                bank = "B%d" % (ring[0] % 2)
+                bank = CFG["ring"][ring[0] % len(CFG["ring"])]
                 ring[0] += 1
+                at(t, tab[0] + "p%d" % ch, AT["tile"] * hk - AT["lead"])
                 for kk in range(8):
                     k = 2 * kk + hk
                     mm(A(bank, kk, 512, 8), A("SW", 128 * k, 128 * k + 128), st("WT", s, b, v, v + 64))
                 o = 512 * ((2 * ch + hk) % 4)
-                tt(A(pbuf, o, o + 512), A(gbuf, 16 * v + hk, 16 * v + 1024, 2), A(bank), ALU.mult)
+                at(t, tab[0] + "p%d" % ch, AT["tile"] * hk)
+                tt(A(pbuf, o, o + 512), A(gbuf, go + hk, go + 1024, 2), A(bank), ALU.mult)
+                at(t, tab[0] + "p%d" % ch, AT["tile"] * hk + AT["lag"])
                 yield ch, hk, o
 
     def xphase(t):
@@ -347,80 +434,155 @@ def build(rank):
                     sends.append(send("XT", t + 2, a, a + 128, a == 0, "ax%d" % (t + 1), LAT["xa" if a == 0 else "xb"]))
         if t < 5:
             arrx[t + 1] = arr("ax%d" % (t + 1), sends)
+        b = t % 2
+        eb, eo = CFG["eb"]
+        mm(A(eb, eo, eo + 256), A("BO"), A("XT", *own(t + 2)))
+        at(t, "str")
+        act(st("STR", 0, b), A(eb, eo, eo + 256), ACT.Sign, A("QB", 3, 4))
         if t >= 4:
-            b = t % 2
             act(A("OX"), A("XT", *own(t + 2)), ACT.Identity)
             store("yx", b * NV, b * NV + NV, A("OX"))
-        mm(A("B3", 256, 512), A("BO"), A("XT", *own(t + 2)))
-        act(A("STR"), A("B3", 256, 512), ACT.Sign, A("QB", 3, 4))
 
     def overlap(t):
         b, s = t % 2, t // 2
         nv = CFG["tile"][t]
         m = 512 // nv
+        cb, co = CFG["cb"]
+        n = 0
         for a in range(0, NV, nv):
+            at(t, "m%d" % (n // 2), -AT["lead"])
+            sc = CFG["abs"][t][a // nv] == "S"
             for j in range(m):
                 mm(A("B2", j, 512, m), idn("one"), A("XT", *own(t, a, a + nv)))
-            mm(A("B5", a, a + nv), idn("p256"), st("NL", s, b, a, a + nv), True, False)
+            if not CFG["ct"]:
+                mm(A(cb, co + a, co + a + nv), idn("p256"), st("NL", s, b, a, a + nv), True, False)
             for kk in range(16 // m):
                 o = 512 * (ring[1] % 4)
                 ring[1] += 1
-                tt(A("MN", o, o + 512), A(CFG["gx"][t], 16 * a + kk, 16 * (a + nv), 16 // m), A("B2"), ALU.min)
+                at(t, "m%d" % (n // 2), AT["tile"] * (n % 2))
+                gx = A(CFG["gx"][t], 16 * a + kk, 16 * (a + nv), 16 // m)
+                last = sc and kk == 16 // m - 1
+                if last:
+                    mm(A("B2"), idn("m1"), gx, True, False)
+                    for j in range(m):
+                        mm(A("B2", j, 512, m), idn("one"), A("XT", *own(t, a, a + nv)), False, j == m - 1)
+                    act(A("MN", o, o + 512), A("B2"), ACT.Relu)
+                else:
+                    tt(A("MN", o, o + 512), gx, A("B2"), ALU.min)
+                at(t, "m%d" % (n // 2), AT["tile"] * (n % 2) + AT["lag"])
+                n += 1
                 for j in range(m):
                     k = kk + 16 // m * j
-                    mm(A("B5", a, a + nv), A("ZZ", 15 - k, 143 - k), A("MN", o + j, o + 512, m), False, k == 15)
-        act(A("KEY"), A("B5", 0, 256), ACT.Identity, -240.0)
-        ts(A("FR"), A("KEY"), A("QB", 2, 3), None, ALU.is_ge)
+                    if CFG["ct"]:
+                        mm(A(cb, co + a + k, co + a + 128, 16), A("MN", o + j, o + 512, m),
+                           A("NB", 0, 8) if last else A("BO", 0, 128, 16))
+                    else:
+                        mm(A(cb, co + a, co + a + nv), A("ZZ", 15 - k, 143 - k), A("MN", o + j, o + 512, m), False, k == 15)
+            if CFG["ct"]:
+                at(t, "key", -1.0)
+                act(A("CT", a, a + 128), A(cb, co + a, co + a + 128), ACT.Identity)
+        if CFG["ct"]:
+            cb, co = CFG["kb"]
+            for a in (0, 128):
+                lin(A(cb, co + a, co + a + 128), [(idn("p256"), st("NL", s, b, a, a + 128))]
+                    + [(A("BM"), A("XT", *own(t, a, a + 128)))] * (CFG["abs"][t][a // nv] == "S")
+                    + [(A("CT", a, a + 128), idn("one"))])
+        at(t, "key")
+        act(st("KEY", 0, b), A(cb, co, co + 256), ACT.Identity, -240.0)
+        at(t, "fr")
+        ts(st("FR", 0, b), st("KEY", 0, b), A("QB", 2, 3), None, ALU.is_ge)
+
+    def spread(t):
+        b, s = t % 2, t // 2
+        for ch in range(4):
+            if CFG["UT"][t][ch] == "F":
+                for hk in range(2):
+                    bank = CFG["wb"][hk]
+                    at(t, "wc", AT["tile"] * (ch + hk) - AT["lead"])
+                    for kk in range(8):
+                        k = 2 * kk + hk
+                        mm(A(bank, kk, 512, 8), A("SW", 128 * k, 128 * k + 128), st("WT", s, b, 64 * ch, 64 * ch + 64))
+                    at(t, "wc", AT["tile"] * (ch + hk))
+                    act(A("WS", 1024 * (ch // 2) + hk, 1024 * (ch // 2) + 1024, 2), A(bank), ACT.Identity)
 
     def uphase(t):
         sends = []
+        spread(t)
         for ch, hk, o in products(t, "UT", "GU", "PU", [arru[t]] if t in arru else []):
             v = 64 * ch
-            bank = "B4" if ch < 2 else "B3"
-            r = A(bank, v % 128, v % 128 + 64)
-            if hk == 0:
+            bank, ro = CFG["rb"][ch % 2 if t < 5 else ch // 2]
+            r = A(bank, ro + v % 128, ro + v % 128 + 64)
+            if hk != 1:
                 mm(r, idn("p128"), A("XT", *own(t, v, v + 64)), True, False)
                 mm(r, A("IF", 128, 256), A("UT", *own(t, v, v + 64)), False, False)
-            if ch in CFG["scan"][t]:
+            if hk == 2:
+                hk = 1
+                if CFG["scan"][t][2 * ch] == "s":
+                    scan(A("PS"), A("SEH"), A("PU", o, o + 1024))
+                    mm(r, A("IF", 0, 128), A("PS", 15, 1024, 16), False, True)
+                else:
+                    for k in range(16):
+                        mm(r, A("IF", 0, 128), A("PU", o + k, o + 1024, 16), False, k == 15)
+            elif CFG["scan"][t][2 * ch + hk] == "s":
                 scan(A("PS", 512 * hk, 512 * hk + 512), A("SEG"), A("PU", o, o + 512))
                 mm(r, A("IF", 0, 128), A("PS", 512 * hk + 7, 512 * hk + 512, 8), False, hk == 1)
             else:
                 for kk in range(8):
                     mm(r, A("IF", 0, 128), A("PU", o + kk, o + 512, 8), False, hk == 1 and kk == 7)
-            if hk == 1 and ch % 2 == 1:
-                a = v - 64
-                act(A("UT", *own(t + 2, a, a + 128)), A(bank, 0, 128), ACT.Tanh, -0.5, 2.0 ** -11)
-                if t < 5:
-                    sends.append(send("UT", t + 2, a, a + 128, a == 0, "au%d" % (t + 1), LAT["ua" if a == 0 else "ub"]))
+            if hk == 1 and t < 5:
+                at(t, "th%d" % ch)
+                act(A("UT", *own(t + 2, v, v + 64)), r, ACT.Tanh, -0.5, 2.0 ** -11)
+                sends.append(send("UT", t + 2, v, v + 64, ch % 2 == 0, "au%d" % (t + 1), LAT["ub" if ch % 2 else "ua"],
+                                  "ab"[ch // 2] + "u%d" % (t + 1)))
+            elif hk == 1 and ch % 2 == 1:
+                at(t, "th%d" % ch)
+                act(A("UT", *own(t + 2, v - 64, v + 64)), A(bank, ro, ro + 128), ACT.Tanh, -0.5, 2.0 ** -11)
         if t < 5:
             arru[t + 1] = arr("au%d" % (t + 1), sends)
         if t >= 4:
             b = t % 2
             store("yu", b * NV, b * NV + NV, A("UT", *own(t + 2)))
 
+    def settle(t, u):
+        b, s = t % 2, t // 2
+        at(t, "gg", AT["P"] * (s == 0))
+        tt(u, u, st("DG", 0, b), ALU.mult)
+        tt(st("GG", s + 1, b), u, st("GG", s, b), ALU.add)
+
     def update(t):
         b, s = t % 2, t // 2
-        nl, nn = st("NL", s, b), st("NL", s + 1, b)
+        nl, nn, fr = st("NL", s, b), st("NL", s + 1, b), st("FR", 0, b)
         for j in range(4):
             bank = CFG["ad"][j % 2]
+            at(t, "sd%d" % j, -AT["lead"])
             for e in range(2):
-                mm(A(bank, 256 * e, 256 * e + 256), ad(2 * j + e + 1), A("KEY"))
+                mm(A(bank, 256 * e, 256 * e + 256), ad(2 * j + e + 1), st("KEY", 0, b))
+            at(t, "sd%d" % j)
             for e in range(2):
                 d = 2 * j + e
                 act(A("SD", 256 * d, 256 * d + 256), A(bank, 256 * e, 256 * e + 256), ACT.Sign, A("THR", d, d + 1))
-        z = A("B7", 0, 256)
-        lin(z, [(A("LM"), nl), (A("NM"), A("STR"))]
+        at(t, "z")
+        z = A(CFG["zb"], 0, 256)
+        lin(z, [(A("LM"), nl), (A("NM"), st("STR", 0, b))]
             + [(ad(15 - d) if d < 7 else idn("m1"), A("SD", 256 * d, 256 * d + 256)) for d in range(8)])
-        ts(A("CAP"), z, 40.0, None, ALU.is_gt)
+        at(t, "cap")
+        sg = CFG["cap"][t] == "S"
+        if sg:
+            act(A("CAP"), z, ACT.Sign, -40.5)
+        else:
+            ts(A("CAP"), z, 40.0, None, ALU.is_gt)
         p, q = A("B6", 0, 256), A("B7", 256, 512)
         rn = st("RR", s + 1, b)
-        lin(p, [(idn("one"), st("RR", s, b)), (idn("p4"), A("FR")), (idn("m3"), A("CAP"))])
-        lin(q, [(idn("one"), st("WW", s, b)), (idn("p4"), A("CAP"))])
+        lin(p, [(idn("one"), st("RR", s, b)), (idn("p4"), fr), (idn("m15" if sg else "m3"), A("CAP"))])
+        lin(q, [(idn("one"), st("WW", s, b)), (idn("p2" if sg else "p4"), A("CAP"))])
+        at(t, "rr")
         if CFG["r"] == "S":
-            act(rn, p, ACT.Relu, -1.0)
+            act(rn, p, ACT.Relu, -2.5 if sg else -1.0)
         else:
-            ts(rn, p, -1.0, 0.0, ALU.add, ALU.max)
-        ts(st("WW", s + 1, b), q, 15.0, None, ALU.min)
+            ts(rn, p, -2.5 if sg else -1.0, 0.0, ALU.add, ALU.max)
+        at(t, "ww")
+        ts(st("WW", s + 1, b), q, 2.0 if sg else 0.0, 15.0, ALU.add, ALU.min)
+        at(t, "nl")
         if CFG["nl"] == "S":
             act(nn, rn, ACT.Relu, 1.0, -1.0)
         else:
@@ -429,14 +591,17 @@ def build(rank):
         c, cn = (st("CC", s, b), st("CC", s + 1, b)) if s < 2 else (st("CF", 1, b), st("CF", 0, b))
 
         def ended(out, f):
-            lin(out, [(idn("m1"), nl), (idn(f), A("FR")), (idn("m1"), A("CAP")), (idn("one"), nn)])
+            lin(out, [(idn("mh"), A("ONE"))] * sg
+                + [(idn("m1"), nl), (idn(f), fr), (idn("mh" if sg else "m1"), A("CAP")), (idn("one"), nn)])
         p, u, w = A("B7", 0, 256), A("B6", 0, 256), A("B6", 256, 512)
+        at(t, "cn")
         if s == 0:
+            u = A("B4", 256, 512)
             ended(u, "p2")
             tt(w, u, d0, ALU.mult)
             tt(cn, w, c, ALU.add)
         else:
-            mm(p, idn("one"), A("FR"))
+            mm(p, idn("one"), fr)
             tt(p, p, st("GG", s, b), ALU.mult)
             tt(A("TA"), p, c, ALU.add)
             ended(w, "one")
@@ -445,11 +610,12 @@ def build(rank):
             tt(w, w, d0, ALU.mult)
             tt(cn, w, A("TA"), ALU.add)
         if s < 2:
+            at(t, "wt")
             weights(s + 1, b, A("B7", 0, 256))
+            at(t, "of")
             columns(s + 1, b, A("B7", 256, 512))
-            tt(u, u, st("DG", 0, b), ALU.mult)
-            tt(st("GG", s + 1, b), u, st("GG", s, b), ALU.add)
             if s == 1:
+                settle(t, u)
                 ts(st("CF", 1, b), cn, 2048.0, None, ALU.add)
         else:
             store("yc", b * NV, b * NV + NV, cn)
@@ -462,11 +628,15 @@ def build(rank):
     jump(0, 1)
     for t in range(6):
         xphase(t)
-        overlap(t)
-        for b in range(2):
-            if CFG["jat"][b] == t:
-                jump(1, b)
-        uphase(t)
+        for ph in CFG["seq"]:
+            if ph == "j":
+                for b in range(2):
+                    if CFG["jat"][b] == t:
+                        jump(1, b)
+            else:
+                (overlap if ph == "o" else uphase)(t)
+        if t in (1, 2):
+            settle(t - 1, A("B4", 256, 512))
         update(t)
     return ops
 
@@ -480,8 +650,10 @@ def schedule(ops):
     lev = [0.0] * n
     for i in range(n - 1, -1, -1):
         o = ops[i]
-        lev[i] = o["cost"] + max([lev[j] + (o["lat"] + HOP if ops[j]["deps"][i] else 0.0) for j in succ[i]] + [o["lat"]])
-    gap = [dict((d, ops[d]["lat"] + HOP if w else 0.0) for d, w in o["deps"].items()) for o in ops]
+        lev[i] = -o["when"] if o["when"] is not None else AT["early"] + o["cost"] + max(
+            [lev[j] + (o["lat"] + HOP if ops[j]["deps"][i] else 0.0) for j in succ[i]] + [-1e9])
+    gap = [dict((d, ops[d]["lat"] * (TIGHT if ops[d]["kind"] == "send" else 1) + HOP if w else 0.0)
+                for d, w in o["deps"].items()) for o in ops]
     back = [dict((j, gap[j][i]) for j in succ[i]) for i in range(n)]
 
     def place(before, after, first, prio):
@@ -496,9 +668,12 @@ def schedule(ops):
         while len(order) < n:
             t, e = min((max(free[e], min(rdy[i] for i in pool[e])), e) for e in pool if pool[e])
             i = min((j for j in pool[e] if rdy[j] <= t + 1e-9), key=lambda j: prio[j])
+            j = min((j for j in pool[e] if rdy[j] <= t + AHEAD * ops[i]["cost"] + 1e-9), key=lambda j: prio[j])
+            if prio[j][0] < prio[i][0] - URGENT:
+                i = j
             pool[e].remove(i)
             order.append(i)
-            free[e] = end[i] = t + ops[i]["cost"]
+            free[e] = end[i] = max(t, rdy[i]) + ops[i]["cost"]
             for j, w in after[i].items():
                 rdy[j] = max(rdy[j], end[i] + w)
                 left[j] -= 1
@@ -506,22 +681,57 @@ def schedule(ops):
                     pool[ops[j]["eng"]].append(j)
         return end, order
 
+    eng = [o["eng"] for o in ops]
+    cases = [([o["cost"] * (fac if o["kind"] in COMPUTE else 1) * (gr if o["kind"] == "gat" else 1) for o in ops],
+              [[(d, ops[d]["lat"] * (lat if ops[d]["kind"] == "send" else 1) + HOP if w else 0.0)
+                for d, w in o["deps"].items()] for o in ops], fac) for gr, fac, lat in CASES]
+
+    def replay(order):
+        total = 0.0
+        for cost, before, fac in cases:
+            free, end = dict((e, 0.0) for e in eng), [0.0] * n
+            for i in order:
+                t = free[eng[i]]
+                for d, w in before[i]:
+                    if end[d] + w > t:
+                        t = end[d] + w
+                end[i] = free[eng[i]] = t + cost[i]
+            total += max(end[i] + tail[i] for i in range(n) if tail[i]) / fac
+        return total / len(cases)
+
     zero, tail = [0.0] * n, [o["lat"] if o["kind"] == "store" else 0.0 for o in ops]
-    best, r = None, SEED
-    for _ in range(ROUNDS):
+    best, r = None, [SEED]
+
+    def draw():
+        r[0] = (r[0] * 1103515245 + 12345) % 2147483648
+        return r[0] / 2147483648
+
+    for k in range(ROUNDS):
         end, order = place(gap, back, zero, [(-lev[i], i) for i in range(n)])
-        length = max(end[i] + tail[i] for i in range(n))
+        length = replay(order)
         if best is None or length < best[0]:
-            best = (length, order)
+            best = (length, order, end)
+        if k % RESTART == RESTART - 1:
+            end = best[2]
         lev = place(back, gap, tail, [(-end[i], -i) for i in range(n)])[0]
         for i in range(n):
-            r = (r * 1103515245 + 12345) % 2147483648
-            lev[i] += SHAKE * r / 2147483648
+            lev[i] += SHAKE * draw()
+    for k in range(TRIES):
+        a, w, s = 135 * draw() - 5, (4, 8, 16)[k % 3], (0.6, 1.6, 4.0)[k // 3 % 3]
+        end = [e + s * (draw() + draw() - 1) if a <= e < a + w and o["eng"] != "P" else e for e, o in zip(best[2], ops)]
+        if k % 2:
+            lev = place(back, gap, tail, [(-end[i], -i) for i in range(n)])[0]
+        else:
+            lev = [ops[i]["cost"] - end[i] for i in range(n)]
+        end, order = place(gap, back, zero, [(-lev[i], i) for i in range(n)])
+        length = replay(order)
+        if length <= best[0]:
+            best = (length, order, end)
     ops[0]["span"] = best[0]
     return best[1]
 
 
-COMPUTE = ("ts", "tt", "cp", "ms", "scan", "act", "gat", "mm", "iota", "sel")
+COMPUTE = ("ts", "tt", "cp", "ms", "scan", "act", "gat", "gtt", "mm", "iota", "sel")
 
 
 def routes(T, topo):
@@ -568,17 +778,17 @@ def rank_program(g, core, T, topo):
     sends = [ops[i]["args"] for i in order if ops[i]["kind"] == "send"]
     total = 0
     if core == out[me]:
-        for tab, lo, hi, via, sem in sends:
+        for tab, lo, hi, via, sem, hop in sends:
             if via:
-                g.wait_ge(T.sem[sem], len(inner))
-                total += fused(g, T, topo, [(land[me, True], outer, T[tab][:, lo:hi], T.sem[sem])])
+                g.wait_ge(T.sem[hop], len(inner))
+                total += fused(g, T, topo, [(land[me, True], outer, T[tab][:, lo:hi], T.sem[hop])])
     elif core != me:
         to = [c for c in T.cores if topo.chip(c) == topo.chip(core) or topo.mates(topo.chip(c), topo.chip(core))]
         eng = topo.engines(core, to[0])
         for j in range(0, len(sends), 2):
             mine = [s for s in sends[j:j + 2] if core in land[me, s[3]]]
             tab, sem = mine[0][0], T.sem[mine[0][4]]
-            g.wait_ge(sem, len(mine) * len(outer))
+            g.wait_ge(T.sem[mine[0][5]], len(mine) * len(outer))
             if mine[0][2] == mine[-1][1]:
                 mine = [(tab, mine[0][1], mine[-1][2])]
             n = len(eng) // len(mine)
@@ -631,7 +841,7 @@ def rank_program(g, core, T, topo):
         elif ops[i]["kind"] in ("load", "store"):
             value[i] = (chan[i], 16)
         elif ops[i]["kind"] == "arr":
-            value[i] = (chan[i], arrivals)
+            value[i] = (chan[i], arrivals * len(ops[i]["deps"]) // 2)
 
     Q = {"V": g.vector, "S": g.scalar, "P": g.tensor, "G": g, "Y": g.sync}
 
@@ -647,12 +857,12 @@ def rank_program(g, core, T, topo):
         for d in waits[i]:
             q.wait_ge(T.sem[value[d][0]], value[d][1])
         if k == "send":
-            tab, lo, hi, via, sem = a
-            a, s = T[tab][:, lo:hi], T.sem[sem]
+            tab, lo, hi, via, sem, hop = a
+            a, s, h = T[tab][:, lo:hi], T.sem[sem], T.sem[hop]
             if via:
-                total += fused(g, T, topo, [([out[me]], inner, a, s), ([sib], outer, a, s)])
+                total += fused(g, T, topo, [([out[me]], inner, a, h), ([sib], outer, a, s)])
             else:
-                total += fused(g, T, topo, [(land[me, False], outer, a, s), ([sib], inner, a, s)])
+                total += fused(g, T, topo, [(land[me, False], outer, a, h), ([sib], inner, a, s)])
             continue
         if k == "ts":
             ins = (q.tensor_scalar(ap(a[0]), ap(a[1]), ap(a[2]), None, a[4]) if a[5] is None
@@ -670,13 +880,15 @@ def rank_program(g, core, T, topo):
         elif k == "gat":
             src = ap(a[1]).indirect(ap(a[2]))
             ins = q.tensor_copy(ap(a[0]), src) if o["eng"] == "V" else q.activation(ap(a[0]), src, ACT.Copy)
+        elif k == "gtt":
+            ins = q.tensor_tensor(ap(a[0]), ap(a[1]).indirect(ap(a[2])), ap(a[3]), ALU.mult)
         elif k == "mm":
             ins = q.matmul(ap(a[0]), ap(a[1]), ap(a[2]), a[3], a[4])
         elif k == "iota":
             ins = (q.iota(ap(a[0]), a[1], a[2], a[3], allow_small_or_imprecise_dtypes=True) if a[4]
                    else q.iota(ap(a[0]), a[1], a[2], a[3]))
         elif k == "sel":
-            ins = q.affine_select(ap(a[0]), ap(a[1]), a[2], a[3], a[4], 0, 1)
+            ins = q.affine_select(ap(a[0]), ap(a[1]), a[2], a[3], a[4], a[5], a[6])
         elif k == "load":
             ins = q.dma_start(ap(a[0]), T[a[1]][:, a[2]:a[3]])
         else:

from concourse.bass import DstId, RemoteDMATransfer
from concourse.mybir import AluOpType as ALU, ActivationFunctionType as ACT

NV = 256
SEQ = 2048
NCORES = 128
CFG = {
    "scan": ("msmsmsms",) * 6,
    "jump": (("S4",), ("V2", "V1", "S1"), ("S1", "S1", "S1", "V1"), ("S1", "S1", "S1", "V1")),
    "jat": (0, 1),
    "tile": (128, 128, 128, 128, 128, 128),
    "r": "S", "nl": "S", "dk": "G" * 8 + "S" * 8, "sw": "V" * 8 + "G" * 8, "ct": True,
    "late": ("p256", "m3", "p4", "m1", "p2", "m16", "m15", "mh"), "ids": (), "cap": "SSSSSS", "pj": True,
    "gx": ("GX", "GX", "GJ", "GK", "GX", "GJ"),
    "ad": ("B6", "B7"), "jb": "B7", "ring": ("B0", "B1"), "rb": (("B4", 0), ("B3", 0)), "cb": ("B5", 0), "kb": ("B5", 256),
    "XT": ("SSSS",) * 6, "UT": ("SSSS",) * 6, "wb": ("B0", "B1"), "abs": ("VV",) * 6,
    "eb": ("B3", 256), "seq": "oju", "zb": "B6",
}
AT = {"early": 3.0, "T0": 16.0, "P": 16.5, "tile": 0.5, "lead": 0.7, "lag": 0.5,
      "Xg0": 0.0, "Xg1": 1.4, "Xg2": 5.5, "Xg3": 6.9, "Xp0": 2.3, "Xp1": 3.3, "Xp2": 6.9, "Xp3": 8.3,
      "Ug0": 8.3, "Ug1": 9.7, "Ug2": 11.1, "Ug3": 12.5, "Up0": 9.7, "Up1": 11.1, "Up2": 12.6, "Up3": 14.0,
      "th0": 11.1, "th1": 12.5, "th2": 13.9, "th3": 15.8, "str": 14.2, "m0": 4.4, "m1": 5.4, "m2": 15.5, "m3": 16.5,
      "key": 19.3, "fr": 19.7, "sd0": 19.7, "sd1": 20.3, "sd2": 20.9, "sd3": 21.5, "z": 22.0, "cap": 22.5, "rr": 23.4,
      "ww": 23.4, "nl": 23.9, "cn": 24.3, "wt": 25.0, "of": 25.3, "gg": 26.0,
      "j0": 8.0, "j1": 10.0, "j2": 22.0, "j3": 30.0, "jp": 1.4}

F, BF, H, I32, U16 = "float32", "bfloat16", "float16", "int32", "uint16"
IDN = {"one": 1.0, "p256": 256.0, "m3": -3.0, "p4": 4.0, "m1": -1.0, "p2": 2.0, "p3": 3.0, "p128": 128.0,
       "m16": -16.0, "m15": -1.5, "mh": -0.5, "h0": 1792.0, "q0": -3840.0, "h1": -2304.0, "q1": 4352.0}
IDK = list(IDN)
MAGIC = 12582912.0
SCRATCH = {
    "XT": ("sbuf", [128, 7 * SEQ + NV], BF), "UT": ("sbuf", [128, 7 * SEQ + NV], F),
    "AX": ("sbuf", [128, 4096], BF),
    "GX": ("sbuf", [128, 4096], BF), "GU": ("sbuf", [128, 4096], F), "GJ": ("sbuf", [128, 4096], BF),
    "GK": ("sbuf", [128, 4096], BF),
    "PX": ("sbuf", [128, 2048], H), "PU": ("sbuf", [128, 2048], F), "PS": ("sbuf", [128, 1024], F),
    "MN": ("sbuf", [128, 2048], BF), "SD": ("sbuf", [128, 2048], BF),
    "S0": ("sbuf", [128, 512], I32), "P0": ("sbuf", [128, 512], I32), "AG": ("sbuf", [128, 512], BF),
    "TH": ("sbuf", [128, 4], I32), "QB": ("sbuf", [128, 8], F),
    "WW": ("sbuf", [128, 2048], BF), "RR": ("sbuf", [128, 2048], BF), "NL": ("sbuf", [128, 2048], BF),
    "LV": ("sbuf", [128, 512], BF), "WT": ("sbuf", [128, 1536], BF),
    "CC": ("sbuf", [128, 1536], H), "CF": ("sbuf", [128, 1024], F), "GG": ("sbuf", [128, 1536], F),
    "D0": ("sbuf", [128, 512], F),
    "DG": ("sbuf", [128, 512], F), "TT": ("sbuf", [128, 512], F), "NC": ("sbuf", [128, 512], H),
    "TA": ("sbuf", [128, 256], F), "TW": ("sbuf", [128, 256], BF), "JC": ("sbuf", [128, 256], H), "SC": ("sbuf", [128, 512], H),
    "OF": ("sbuf", [128, 1536], U16), "OJ": ("sbuf", [128, 1024], U16),
    "NB": ("sbuf", [128, 16], BF), "BM": ("sbuf", [128, 128], BF),
    "HQ": ("sbuf", [128, 512], BF), "CT": ("sbuf", [128, 256], BF),
    "KEY": ("sbuf", [128, 512], BF), "FR": ("sbuf", [128, 512], BF), "CAP": ("sbuf", [128, 256], BF),
    "STR": ("sbuf", [128, 512], BF), "NUL": ("sbuf", [128, 128], BF), "I16": ("sbuf", [128, 128], BF), "OX": ("sbuf", [128, 256], F), "OW": ("sbuf", [128, 256], F),
    "pI": ("sbuf", [128, 8], I32), "COL": ("sbuf", [128, 8], F), "rowm": ("sbuf", [128, 160], F),
    "rowh": ("sbuf", [128, 128], F), "rowl": ("sbuf", [128, 128], F),
    "ONE": ("sbuf", [128, 256], BF), "CST": ("sbuf", [128, 256], BF), "SEG": ("sbuf", [128, 512], BF),
    "YY": ("sbuf", [128, 8, 32], BF),
    "ID": ("sbuf", [128, 128 * len(IDK)], BF), "IH": ("sbuf", [128, 384], H), "IF": ("sbuf", [128, 256], F),
    "KD": ("sbuf", [128, 128], BF), "BO": ("sbuf", [128, 128], BF), "ZZ": ("sbuf", [128, 144], BF),
    "NM": ("sbuf", [128, 128], BF), "LM": ("sbuf", [128, 128], BF), "KM": ("sbuf", [128, 256], BF),
    "MK": ("sbuf", [128, 32], F), "THR": ("sbuf", [128, 16], F),
    "SW": ("sbuf", [128, 2048], BF), "DK": ("sbuf", [128, 2048], BF), "AD": ("sbuf", [128, 2048], BF),
}
for _b in range(8):
    SCRATCH["B%d" % _b] = ("psum", [128, 512], F)
NDMA = 20
SEMAPHORES = (["cV", "cS", "cP", "cG", "sent"] + ["ax%d" % j for j in range(6)] + ["au%d" % j for j in range(6)]
              + ["bu%d" % j for j in range(1, 6)] + ["d%d" % j for j in range(NDMA)])

CY, PC, GR, HOP = 0.00083, 0.00043, 1.56, 0.17
ROUNDS, SEED, SHAKE, RESTART, AHEAD, URGENT, TIGHT = 16, 3, 0.3, 8, 1.0, 0.5, 0.95
TRIES = 500
CASES = ((1, 1, 1), (1, 1.4, 1), (0.72, 1.15, 1), (1.25, 1.2, 1.1))
ORDER = []
LAT = {"xa": 8.3, "xb": 5.8, "ua": 8.7, "ub": 6.7, "x0": 11.5, "u0": 17.0}


def span(shape, idx):
    lo = hi = 0
    n = 1
    st = 1
    for d in range(len(shape) - 1, 0, -1):
        e = idx[d] if d < len(idx) else slice(None)
        if isinstance(e, slice):
            r = range(*e.indices(shape[d]))
            lo += r[0] * st
            hi += r[-1] * st
            n *= len(r)
        else:
            lo += e * st
            hi += e * st
        st *= shape[d]
    return lo, hi + 1, n


def A(name, a=None, b=None, s=None):
    return (name, (slice(None), slice(a, b, s)))


def A3(name, a, b, c, d=None):
    return (name, (slice(None), slice(a, b), c if d is None else slice(c, d)))


def build(rank):
    ops = []
    hist = {}
    now = [None]

    def info(x):
        where, shape, dt = SCRATCH[x[0]]
        lo, hi, n = span(shape, x[1])
        return where, lo, hi, n, dt

    def add(eng, kind, args, reads, writes, cost, extra=(), lat=0.0):
        i = len(ops)
        deps = {}
        for d in extra:
            deps[d] = True
        seen = set()
        for x, w in [(x, True) for x in writes] + [(x, False) for x in reads]:
            where, lo, hi, n, dt = info(x)
            if where == "psum":
                wr = any(y[0] == x[0] for y in writes)
                if x[0] in seen:
                    continue
                seen.add(x[0])
                if x[0] in hist:
                    j, jw = hist[x[0]]
                    same = ops[j]["eng"] == eng
                    need = not (same and (eng == "P" or (not jw and not wr)))
                    deps[j] = deps.get(j, False) or need
                hist[x[0]] = (i, wr)
                continue
            h = hist.setdefault(x[0], [])
            keep = []
            for e in h:
                j, l2, h2, w2 = e
                if j != i and l2 < hi and lo < h2 and (w or w2):
                    deps[j] = True
                if j != i and w and n == hi - lo and lo <= l2 and h2 <= hi:
                    continue
                keep.append(e)
            keep.append((i, lo, hi, w))
            hist[x[0]] = keep
        if kind in ("load", "send", "iota"):
            if (eng, kind != "load") in hist:
                deps.setdefault(hist[eng, kind != "load"], False)
            hist[eng, kind != "load"] = i
        ops.append({"eng": eng, "kind": kind, "args": args, "deps": deps, "cost": cost, "lat": lat, "when": now[0]})
        return i

    def isap(x):
        return isinstance(x, tuple)

    def two(*xs):
        return all(info(x)[4] in (BF, H, U16) for x in xs)

    def vc(n):
        return 0.05 + max(64, n) * CY

    def ts(out, in0, s1, s2, op0, op1=None):
        n = info(out)[3]
        return add("V", "ts", (out, in0, s1, s2, op0, op1), [in0] + [s for s in (s1, s2) if isap(s)], [out],
                   vc(n * (0.5 if two(out, in0) else 1)))

    def tt(out, a, b, op):
        n = info(out)[3]
        return add("V", "tt", (out, a, b, op), [a, b], [out],
                   vc(n * (2 if info(a)[0] == "sbuf" and info(b)[0] == "sbuf" else 1)))

    def cp(out, a):
        return add("V", "cp", (out, a), [a], [out], vc(info(out)[3] * (0.5 if two(out, a) else 1)))

    def ms(out, c):
        return add("V", "ms", (out, c), [], [out], vc(info(out)[3] * 0.5))

    def scan(out, a, b):
        return add("V", "scan", (out, a, b), [a, b], [out], vc(info(out)[3]))

    def act(out, a, f, bias=0.0, scale=1.0):
        return add("S", "act", (out, a, f, bias, scale), [a] + [s for s in (bias, scale) if isap(s)], [out],
                   0.065 + max(64, info(out)[3]) * CY)

    def gat(eng, out, win, off, extra=()):
        return add(eng, "gat", (out, win, off), [win, off], [out], 0.06 + info(out)[3] * GR * CY, extra)

    def mm(out, l, r, st=True, sp=True):
        return add("P", "mm", (out, l, r, st, sp), [l, r], [out],
                   max(64, info(out)[3]) * PC * (4 if info(r)[4] == F else 1))

    def lin(out, terms):
        for j, (l, r) in enumerate(terms):
            mm(out, l, r, j == 0, j == len(terms) - 1)

    def load(q, out, name, a, b, lat):
        return add(q, "load", (out, name, a, b), [], [out], 0.1, lat=lat)

    def store(name, a, b, src):
        return add("Y", "store", (src, name, a, b), [src], [], 0.1, lat=2.0)

    def idn(k):
        j = IDK.index(k)
        return A("ID", 128 * j, 128 * j + 128)

    def own(j, a=0, b=NV):
        o = j * SEQ + (rank * NV if j < 7 else 0)
        return o + a, o + b

    def send(tab, j, a, b, via, sem, lat, hop=None):
        lo, hi = own(j, a, b)
        return add("G", "send", (tab, lo, hi, via, sem, hop or sem), [A(tab, lo, hi)], [], 0.5, lat=lat)

    def arr(sem, sends):
        return add("A", "arr", (sem,), [], [], 0.0, extra=sends)

    def st(name, stage, b, a=0, e=NV):
        o = stage * 512 + b * NV
        return A(name, o + a, o + e)

    for b in range(2):
        load("YS"[b], A("XT", *own(b)), "x0", b * NV, b * NV + NV, 2.2)
    load("Y", A("S0"), "s0", 0, 512, 2.6)
    load("S", A("P0"), "p0", 0, 512, 2.8)
    load("Y", A("AG"), "ag", 0, 512, 3.0)
    load("S", A("WW", 0, 512), "w0", 0, 512, 3.2)
    load("Y", A("TH", 0, 2), "th", 0, 2, 3.2)
    for b in range(2):
        load("SY"[b], A("UT", *own(b)), "u0", b * NV, b * NV + NV, 3.8)
    load("Y", A("AX"), "ax", 0, 4096, 7.0)
    add("G", "iota", (A("pI", 0, 1), [[0, 1]], 0, 1, False), [], [A("pI", 0, 1)], 0.14)
    add("G", "iota", (A("rowm"), [[1, 160]], 0, 0, True), [], [A("rowm")], 0.4)
    add("G", "iota", (A("rowh"), [[16, 8], [0, 16]], 0, 0, True), [], [A("rowh")], 0.35)
    add("G", "iota", (A("rowl"), [[0, 8], [1, 16]], 0, 0, True), [], [A("rowl")], 0.35)
    arrx = {0: arr("ax0", [send("XT", 0, 0, NV, True, "ax0", LAT["x0"]), send("XT", 1, 0, NV, False, "ax0", LAT["x0"] - 2)])}
    arru = {0: arr("au0", [send("UT", 0, 0, NV, True, "au0", LAT["u0"]), send("UT", 1, 0, NV, False, "au0", LAT["u0"] - 2)])}

    pc, kc, gc = A("COL", 0, 1), A("COL", 1, 2), A("COL", 2, 3)
    ms(A("ONE"), 1.0)
    ms(A("CST", 0, 128), -255.0 / 512)
    ms(A("CST", 128, 256), MAGIC)
    ts(A("pI", 1, 2), A("pI", 0, 1), 15, None, ALU.bitwise_and)
    ts(A("pI", 2, 3), A("pI", 0, 1), 112, None, ALU.bitwise_and)
    cp(A("COL", 0, 3), A("pI", 0, 3))
    ts(idn("one"), A("rowm", 0, 128), pc, None, ALU.is_equal)
    behind = hist["G", True]

    def sel(out, src, pattern, op, fill, base=0, cm=1):
        j = add("G", "sel", (out, src, pattern, op, fill, base, cm), [src], [out], 0.17 + 2 * CY * info(out)[3])
        ops[j]["deps"].setdefault(behind, False)

    if CFG["late"]:
        ms(A("NUL"), 0.0)
    for k in IDK[1:]:
        if k in CFG["late"]:
            sel(idn(k), A("NUL"), [[-1, 128]], ALU.not_equal, IDN[k])
        elif k in CFG["ids"]:
            act(idn(k), idn("one"), ACT.Identity, 0.0, IDN[k])
        else:
            ts(idn(k), idn("one"), IDN[k], None, ALU.mult)
    ts(A("IH", 0, 128), idn("one"), 1.0 / 256, None, ALU.mult)
    ts(A("IH", 128, 256), idn("one"), 1.0, None, ALU.mult)
    ts(A("IH", 256, 384), idn("one"), -1.0, None, ALU.mult)
    act(A("IF", 0, 128), idn("one"), ACT.Identity)
    act(A("IF", 128, 256), idn("one"), ACT.Identity, 0.0, 1024.0)
    act(A("KD"), idn("one"), ACT.Identity, 0.0, kc)
    ts(A("BO"), A("rowh"), gc, None, ALU.is_equal)
    if not CFG["ct"]:
        ts(A("ZZ"), A("rowm", 0, 144), -15.0, gc, ALU.add, ALU.is_equal)
    act(A("NB", 0, 8), A("BO", 0, 128, 16), ACT.Identity, 0.0, -1.0)
    sel(A("BM"), A("BO"), [[0, 32], [1, 4]], ALU.is_equal, 0.0, -3, 0)
    ts(A("MK", 0, 16), A("rowm", 0, 16), kc, None, ALU.is_equal)
    ts(A("MK", 16, 32), A("MK", 0, 16), 16.0, None, ALU.mult)
    if "G" in CFG["dk"]:
        act(A("I16"), idn("one"), ACT.Identity, 0.0, 16.0)
    for k in range(16):
        o = A("DK", 128 * k, 128 * k + 128)
        if CFG["dk"][k] == "S":
            act(o, idn("one"), ACT.Identity, 0.0, A("MK", 16 + k, 17 + k))
        elif CFG["dk"][k] == "V":
            ts(o, idn("one"), A("MK", 16 + k, 17 + k), None, ALU.mult)
        else:
            sel(o, A("I16"), [[0, 8], [1, 16]], ALU.is_equal, 0.0, -k, 0)
    for k in range(16):
        o = A("SW", 128 * k, 128 * k + 128)
        if CFG["sw"][k] == "S":
            act(o, A("BO"), ACT.Identity, 0.0, A("MK", k, k + 1))
        elif CFG["sw"][k] == "V":
            ts(o, A("BO"), A("MK", k, k + 1), None, ALU.mult)
        else:
            sel(o, A("ONE", 0, 128), [[-16, 8], [0, 16]], ALU.is_equal, 0.0, -k, 1)
    ts(A("KM", 0, 128), A("rowl"), kc, None, ALU.is_equal)
    sel(A("NM"), A("KM", 0, 128), [[-1, 128]], ALU.not_equal, 33.0)
    act(A("KM", 128, 256), A("BO"), ACT.Identity, 0.0, 2.0)
    sel(A("LM"), A("KM", 128, 256), [[-1, 128]], ALU.not_equal, -126.0)
    ts(A("THR", 8, 16), A("rowm", 1, 9), kc, 16.0, ALU.add, ALU.is_ge)
    ts(A("THR", 0, 8), A("THR", 8, 16), -0.5, None, ALU.add)
    cp(A("QB", 0, 2), A("TH", 0, 2))
    ts(A("QB", 2, 3), A("QB", 0, 1), 16.0, None, ALU.add)
    ts(A("QB", 3, 4), A("QB", 1, 2), -1.0, 0.5, ALU.mult, ALU.add)
    ms(A("SEG"), 1.0)
    ms(A("SEG", 0, 512, 8), 0.0)
    if any(u[ch] == "F" and c[2 * ch] == "s" for u, c in zip(CFG["UT"], CFG["scan"]) for ch in range(4)):
        ms(A("SEH"), 1.0)
        ms(A("SEH", 0, 1024, 16), 0.0)
    yall = A3("YY", 0, 8, 0, 32)
    sel(yall, A("ONE"), [[-16, 8], [0, 2], [-1, 16]], ALU.is_equal, 0.0)
    for d in list(range(1, 16)):
        sel(A("AD", 128 * d, 128 * d + 128), A3("YY", 0, 8, d, d + 16), [[-1, 128]], ALU.not_equal, -1.0)

    def ad(d):
        return A("AD", 128 * d, 128 * d + 128)

    def columns(stage, b, p):
        c = st("CC", stage, b)
        ts(A("HQ", 0, 256), c, 1.0 / 256, 199.501953125, ALU.mult, ALU.add)
        ts(A("HQ", 256, 512), c, 1.0 / 512, 195.5009765625, ALU.mult, ALU.add)
        lin(p, [(A("IH", 128, 256), c), (idn("h%d" % b), A("HQ", 0, 256)), (idn("q%d" % b), A("HQ", 256, 512))])
        ts(st("OF", stage, b), p, 2048.0 + 393216.0 if b == 0 else 4096.0 - 393216.0, None, ALU.add)

    def weights(stage, b, p):
        lin(p, [(idn("one"), A("ONE")), (idn("one"), st("RR", stage, b)), (idn("p3"), st("NL", stage, b))])
        tt(st("WT", stage, b), p, st("WW", stage, b), ALU.mult)

    def start():
        act(A("NL", 0, 512), A("AG"), ACT.Relu, -2.0)
        act(A("LV"), A("NL", 0, 512), ACT.Identity, 1.0, -1.0)
        act(A("RR", 0, 512), A("AG"), ACT.Identity, 3.0, -1.0)
        p = A("B7")
        tt(p, A("P0"), A("S0"), ALU.subtract)
        tt(p, p, A("LV"), ALU.mult)
        tt(A("CF", 0, 512), p, A("S0"), ALU.add)
        act(A("TT"), p, ACT.Identity)
        cp(A("OJ", 0, 512), A("CF", 0, 512))
        ts(A("CC", 0, 512), A("CF", 0, 512), -2048.0, None, ALU.add)
        if CFG["pj"]:
            ts(A("SC"), A("S0"), -2048.0, None, ALU.add)
        for b in range(2):
            columns(0, b, A("B4", 0, 256))
            weights(0, b, A("B5", 0, 256))

    def jump(rnd, b):
        gj = "GJ" if b == 0 else "GK"
        ch = 0
        for e, w in CFG["jump"][2 * rnd + b]:
            now[0] = AT["j%d" % (2 * rnd + b)] + AT["jp"] * ch
            gat(e, A(gj, 1024 * ch, 1024 * (ch + int(w))), A("AX"), st("OJ", rnd, b, 64 * ch, 64 * (ch + int(w))))
            ch += int(w)
        p = A(CFG["jb"], 0, 256)
        if CFG["pj"]:
            n = st("CC", 0, b) if rnd == 0 else st("NC", 0, b)
            mm(p, A("KD"), A("ONE"), True, False)
            mm(p, A("IH", 128, 256), n, False, False)
            for k in range(16):
                mm(p, A("DK", 128 * k, 128 * k + 128), A(gj, k, 4096, 16), False, k == 15)
            ts(A("TW"), p, 2048.0, -4096.0, ALU.is_ge, ALU.mult)
            tt(A("JC"), p, A("TW"), ALU.add)
            q, p = p, A(CFG["jb"], 256, 512)
            lin(p, [(A("IH", 256, 384), n), (A("IH", 128, 256), A("JC"))])
            if rnd == 0:
                tt(q, p, st("NL", 0, b), ALU.mult)
                tt(st("NC", 0, b), q, st("SC", 0, b), ALU.add)
                ts(st("OJ", 1, b), st("NC", 0, b), 2048.0, None, ALU.add)
                tt(st("D0", 0, b), q, st("TT", 0, b), ALU.subtract)
                act(st("GG", 0, b), p, ACT.Identity)
            else:
                tt(st("DG", 0, b), p, st("GG", 0, b), ALU.subtract)
            return
        lin(p, [(A("KD"), A("ONE"))] + [(A("DK", 128 * k, 128 * k + 128), A(gj, k, 4096, 16)) for k in range(16)])
        tt(A("TC"), p, n, ALU.add)
        ts(A("TB"), A("TC"), 4096.0, -4096.0, ALU.is_ge, ALU.mult)
        if rnd == 0:
            tt(st("GG", 0, b), p, A("TB"), ALU.add)
            q = A(CFG["jb"], 256, 512)
            mm(q, idn("one"), st("NL", 0, b))
            tt(q, q, st("GG", 0, b), ALU.mult)
            tt(st("N1", 0, b), q, st("S0", 0, b), ALU.add)
            tt(st("D0", 0, b), q, st("TT", 0, b), ALU.subtract)
            cp(st("OJ", 1, b), st("N1", 0, b))
        else:
            tt(p, p, A("TB"), ALU.add)
            tt(st("DG", 0, b), p, st("GG", 0, b), ALU.subtract)

    ring = [0, 0, 0]

    def at(t, name, plus=0.0):
        now[0] = AT["T0"] + AT["P"] * t + AT[name] + plus

    def products(t, tab, gbuf, pbuf, first):
        b, s = t % 2, t // 2
        for ch in range(4):
            v = 64 * ch
            at(t, tab[0] + "g%d" % ch)
            who = CFG[tab][t][ch]
            if who == "F":
                o = 1024 * (ch % 2)
                w = A("WS", 1024 * (ch // 2), 1024 * (ch // 2) + 1024)
                off, win = st("OF", s, b, v, v + 64), A(tab, t * SEQ, t * SEQ + 2 * SEQ)
                at(t, tab[0] + "p%d" % ch)
                add("V", "gtt", (A(pbuf, o, o + 1024), win, off, w), [win, off, w], [A(pbuf, o, o + 1024)],
                    0.06 + 1024 * GR * CY, first)
                at(t, tab[0] + "p%d" % ch, AT["lag"])
                yield ch, 2, o
                continue
            w = 64 // len(who)
            go = 1024 * ch
            for j, e in enumerate(who):
                a = v + w * j
                gat(e, A(gbuf, go + 16 * w * j, go + 16 * w * (j + 1)), A(tab, t * SEQ, t * SEQ + 2 * SEQ),
                    st("OF", s, b, a, a + w), first)
            for hk in range(2):
                bank = CFG["ring"][ring[0] % len(CFG["ring"])]
                ring[0] += 1
                at(t, tab[0] + "p%d" % ch, AT["tile"] * hk - AT["lead"])
                for kk in range(8):
                    k = 2 * kk + hk
                    mm(A(bank, kk, 512, 8), A("SW", 128 * k, 128 * k + 128), st("WT", s, b, v, v + 64))
                o = 512 * ((2 * ch + hk) % 4)
                at(t, tab[0] + "p%d" % ch, AT["tile"] * hk)
                tt(A(pbuf, o, o + 512), A(gbuf, go + hk, go + 1024, 2), A(bank), ALU.mult)
                at(t, tab[0] + "p%d" % ch, AT["tile"] * hk + AT["lag"])
                yield ch, hk, o

    def xphase(t):
        sends = []
        for ch, hk, o in products(t, "XT", CFG["gx"][t], "PX", [arrx[t]] if t in arrx else []):
            v = 64 * ch
            if hk == 0 and ch % 2 == 0:
                mm(A("B3", v, v + 128), idn("one"), A("CST", 0, 128), True, False)
            for kk in range(8):
                mm(A("B3", v, v + 64), A("IH", 0, 128), A("PX", o + kk, o + 512, 8), False, False)
            if hk == 1 and ch % 2 == 1:
                a = v - 64
                mm(A("B3", a, a + 128), idn("one"), A("CST", 128, 256), False, True)
                ts(A("XT", *own(t + 2, a, a + 128)), A("B3", a, a + 128), -MAGIC, 15.0, ALU.add, ALU.min)
                if t < 5:
                    sends.append(send("XT", t + 2, a, a + 128, a == 0, "ax%d" % (t + 1), LAT["xa" if a == 0 else "xb"]))
        if t < 5:
            arrx[t + 1] = arr("ax%d" % (t + 1), sends)
        b = t % 2
        eb, eo = CFG["eb"]
        mm(A(eb, eo, eo + 256), A("BO"), A("XT", *own(t + 2)))
        at(t, "str")
        act(st("STR", 0, b), A(eb, eo, eo + 256), ACT.Sign, A("QB", 3, 4))
        if t >= 4:
            act(A("OX"), A("XT", *own(t + 2)), ACT.Identity)
            store("yx", b * NV, b * NV + NV, A("OX"))

    def overlap(t):
        b, s = t % 2, t // 2
        nv = CFG["tile"][t]
        m = 512 // nv
        cb, co = CFG["cb"]
        n = 0
        for a in range(0, NV, nv):
            at(t, "m%d" % (n // 2), -AT["lead"])
            sc = CFG["abs"][t][a // nv] == "S"
            for j in range(m):
                mm(A("B2", j, 512, m), idn("one"), A("XT", *own(t, a, a + nv)))
            if not CFG["ct"]:
                mm(A(cb, co + a, co + a + nv), idn("p256"), st("NL", s, b, a, a + nv), True, False)
            for kk in range(16 // m):
                o = 512 * (ring[1] % 4)
                ring[1] += 1
                at(t, "m%d" % (n // 2), AT["tile"] * (n % 2))
                gx = A(CFG["gx"][t], 16 * a + kk, 16 * (a + nv), 16 // m)
                last = sc and kk == 16 // m - 1
                if last:
                    mm(A("B2"), idn("m1"), gx, True, False)
                    for j in range(m):
                        mm(A("B2", j, 512, m), idn("one"), A("XT", *own(t, a, a + nv)), False, j == m - 1)
                    act(A("MN", o, o + 512), A("B2"), ACT.Relu)
                else:
                    tt(A("MN", o, o + 512), gx, A("B2"), ALU.min)
                at(t, "m%d" % (n // 2), AT["tile"] * (n % 2) + AT["lag"])
                n += 1
                for j in range(m):
                    k = kk + 16 // m * j
                    if CFG["ct"]:
                        mm(A(cb, co + a + k, co + a + 128, 16), A("MN", o + j, o + 512, m),
                           A("NB", 0, 8) if last else A("BO", 0, 128, 16))
                    else:
                        mm(A(cb, co + a, co + a + nv), A("ZZ", 15 - k, 143 - k), A("MN", o + j, o + 512, m), False, k == 15)
            if CFG["ct"]:
                at(t, "key", -1.0)
                act(A("CT", a, a + 128), A(cb, co + a, co + a + 128), ACT.Identity)
        if CFG["ct"]:
            cb, co = CFG["kb"]
            for a in (0, 128):
                lin(A(cb, co + a, co + a + 128), [(idn("p256"), st("NL", s, b, a, a + 128))]
                    + [(A("BM"), A("XT", *own(t, a, a + 128)))] * (CFG["abs"][t][a // nv] == "S")
                    + [(A("CT", a, a + 128), idn("one"))])
        at(t, "key")
        act(st("KEY", 0, b), A(cb, co, co + 256), ACT.Identity, -240.0)
        at(t, "fr")
        ts(st("FR", 0, b), st("KEY", 0, b), A("QB", 2, 3), None, ALU.is_ge)

    def spread(t):
        b, s = t % 2, t // 2
        for ch in range(4):
            if CFG["UT"][t][ch] == "F":
                for hk in range(2):
                    bank = CFG["wb"][hk]
                    at(t, "wc", AT["tile"] * (ch + hk) - AT["lead"])
                    for kk in range(8):
                        k = 2 * kk + hk
                        mm(A(bank, kk, 512, 8), A("SW", 128 * k, 128 * k + 128), st("WT", s, b, 64 * ch, 64 * ch + 64))
                    at(t, "wc", AT["tile"] * (ch + hk))
                    act(A("WS", 1024 * (ch // 2) + hk, 1024 * (ch // 2) + 1024, 2), A(bank), ACT.Identity)

    def uphase(t):
        sends = []
        spread(t)
        for ch, hk, o in products(t, "UT", "GU", "PU", [arru[t]] if t in arru else []):
            v = 64 * ch
            bank, ro = CFG["rb"][ch % 2 if t < 5 else ch // 2]
            r = A(bank, ro + v % 128, ro + v % 128 + 64)
            if hk != 1:
                mm(r, idn("p128"), A("XT", *own(t, v, v + 64)), True, False)
                mm(r, A("IF", 128, 256), A("UT", *own(t, v, v + 64)), False, False)
            if hk == 2:
                hk = 1
                if CFG["scan"][t][2 * ch] == "s":
                    scan(A("PS"), A("SEH"), A("PU", o, o + 1024))
                    mm(r, A("IF", 0, 128), A("PS", 15, 1024, 16), False, True)
                else:
                    for k in range(16):
                        mm(r, A("IF", 0, 128), A("PU", o + k, o + 1024, 16), False, k == 15)
            elif CFG["scan"][t][2 * ch + hk] == "s":
                scan(A("PS", 512 * hk, 512 * hk + 512), A("SEG"), A("PU", o, o + 512))
                mm(r, A("IF", 0, 128), A("PS", 512 * hk + 7, 512 * hk + 512, 8), False, hk == 1)
            else:
                for kk in range(8):
                    mm(r, A("IF", 0, 128), A("PU", o + kk, o + 512, 8), False, hk == 1 and kk == 7)
            if hk == 1 and t < 5:
                at(t, "th%d" % ch)
                act(A("UT", *own(t + 2, v, v + 64)), r, ACT.Tanh, -0.5, 2.0 ** -11)
                sends.append(send("UT", t + 2, v, v + 64, ch % 2 == 0, "au%d" % (t + 1), LAT["ub" if ch % 2 else "ua"],
                                  "ab"[ch // 2] + "u%d" % (t + 1)))
            elif hk == 1 and ch % 2 == 1:
                at(t, "th%d" % ch)
                act(A("UT", *own(t + 2, v - 64, v + 64)), A(bank, ro, ro + 128), ACT.Tanh, -0.5, 2.0 ** -11)
        if t < 5:
            arru[t + 1] = arr("au%d" % (t + 1), sends)
        if t >= 4:
            b = t % 2
            store("yu", b * NV, b * NV + NV, A("UT", *own(t + 2)))

    def settle(t, u):
        b, s = t % 2, t // 2
        at(t, "gg", AT["P"] * (s == 0))
        tt(u, u, st("DG", 0, b), ALU.mult)
        tt(st("GG", s + 1, b), u, st("GG", s, b), ALU.add)

    def update(t):
        b, s = t % 2, t // 2
        nl, nn, fr = st("NL", s, b), st("NL", s + 1, b), st("FR", 0, b)
        for j in range(4):
            bank = CFG["ad"][j % 2]
            at(t, "sd%d" % j, -AT["lead"])
            for e in range(2):
                mm(A(bank, 256 * e, 256 * e + 256), ad(2 * j + e + 1), st("KEY", 0, b))
            at(t, "sd%d" % j)
            for e in range(2):
                d = 2 * j + e
                act(A("SD", 256 * d, 256 * d + 256), A(bank, 256 * e, 256 * e + 256), ACT.Sign, A("THR", d, d + 1))
        at(t, "z")
        z = A(CFG["zb"], 0, 256)
        lin(z, [(A("LM"), nl), (A("NM"), st("STR", 0, b))]
            + [(ad(15 - d) if d < 7 else idn("m1"), A("SD", 256 * d, 256 * d + 256)) for d in range(8)])
        at(t, "cap")
        sg = CFG["cap"][t] == "S"
        if sg:
            act(A("CAP"), z, ACT.Sign, -40.5)
        else:
            ts(A("CAP"), z, 40.0, None, ALU.is_gt)
        p, q = A("B6", 0, 256), A("B7", 256, 512)
        rn = st("RR", s + 1, b)
        lin(p, [(idn("one"), st("RR", s, b)), (idn("p4"), fr), (idn("m15" if sg else "m3"), A("CAP"))])
        lin(q, [(idn("one"), st("WW", s, b)), (idn("p2" if sg else "p4"), A("CAP"))])
        at(t, "rr")
        if CFG["r"] == "S":
            act(rn, p, ACT.Relu, -2.5 if sg else -1.0)
        else:
            ts(rn, p, -2.5 if sg else -1.0, 0.0, ALU.add, ALU.max)
        at(t, "ww")
        ts(st("WW", s + 1, b), q, 2.0 if sg else 0.0, 15.0, ALU.add, ALU.min)
        at(t, "nl")
        if CFG["nl"] == "S":
            act(nn, rn, ACT.Relu, 1.0, -1.0)
        else:
            ts(nn, rn, 0.0, None, ALU.is_equal)
        d0 = st("D0", 0, b)
        c, cn = (st("CC", s, b), st("CC", s + 1, b)) if s < 2 else (st("CF", 1, b), st("CF", 0, b))

        def ended(out, f):
            lin(out, [(idn("mh"), A("ONE"))] * sg
                + [(idn("m1"), nl), (idn(f), fr), (idn("mh" if sg else "m1"), A("CAP")), (idn("one"), nn)])
        p, u, w = A("B7", 0, 256), A("B6", 0, 256), A("B6", 256, 512)
        at(t, "cn")
        if s == 0:
            u = A("B4", 256, 512)
            ended(u, "p2")
            tt(w, u, d0, ALU.mult)
            tt(cn, w, c, ALU.add)
        else:
            mm(p, idn("one"), fr)
            tt(p, p, st("GG", s, b), ALU.mult)
            tt(A("TA"), p, c, ALU.add)
            ended(w, "one")
            if s == 1:
                ended(u, "p2")
            tt(w, w, d0, ALU.mult)
            tt(cn, w, A("TA"), ALU.add)
        if s < 2:
            at(t, "wt")
            weights(s + 1, b, A("B7", 0, 256))
            at(t, "of")
            columns(s + 1, b, A("B7", 256, 512))
            if s == 1:
                settle(t, u)
                ts(st("CF", 1, b), cn, 2048.0, None, ALU.add)
        else:
            store("yc", b * NV, b * NV + NV, cn)
            lin(p, [(idn("m16"), rn), (idn("one"), st("WW", 3, b))])
            act(A("OW"), p, ACT.Identity, 48.0)
            store("yw", b * NV, b * NV + NV, A("OW"))

    start()
    jump(0, 0)
    jump(0, 1)
    for t in range(6):
        xphase(t)
        for ph in CFG["seq"]:
            if ph == "j":
                for b in range(2):
                    if CFG["jat"][b] == t:
                        jump(1, b)
            else:
                (overlap if ph == "o" else uphase)(t)
        if t in (1, 2):
            settle(t - 1, A("B4", 256, 512))
        update(t)
    return ops


def schedule(ops):
    n = len(ops)
    succ = [[] for _ in range(n)]
    for i, o in enumerate(ops):
        for d in o["deps"]:
            succ[d].append(i)
    lev = [0.0] * n
    for i in range(n - 1, -1, -1):
        o = ops[i]
        lev[i] = -o["when"] if o["when"] is not None else AT["early"] + o["cost"] + max(
            [lev[j] + (o["lat"] + HOP if ops[j]["deps"][i] else 0.0) for j in succ[i]] + [-1e9])
    gap = [dict((d, ops[d]["lat"] * (TIGHT if ops[d]["kind"] == "send" else 1) + HOP if w else 0.0)
                for d, w in o["deps"].items()) for o in ops]
    back = [dict((j, gap[j][i]) for j in succ[i]) for i in range(n)]

    def place(before, after, first, prio):
        left = [len(b) for b in before]
        rdy = list(first)
        pool = dict((o["eng"], []) for o in ops)
        for i in range(n):
            if left[i] == 0:
                pool[ops[i]["eng"]].append(i)
        free = dict((e, 0.0) for e in pool)
        end, order = [0.0] * n, []
        while len(order) < n:
            t, e = min((max(free[e], min(rdy[i] for i in pool[e])), e) for e in pool if pool[e])
            i = min((j for j in pool[e] if rdy[j] <= t + 1e-9), key=lambda j: prio[j])
            j = min((j for j in pool[e] if rdy[j] <= t + AHEAD * ops[i]["cost"] + 1e-9), key=lambda j: prio[j])
            if prio[j][0] < prio[i][0] - URGENT:
                i = j
            pool[e].remove(i)
            order.append(i)
            free[e] = end[i] = max(t, rdy[i]) + ops[i]["cost"]
            for j, w in after[i].items():
                rdy[j] = max(rdy[j], end[i] + w)
                left[j] -= 1
                if left[j] == 0:
                    pool[ops[j]["eng"]].append(j)
        return end, order

    eng = [o["eng"] for o in ops]
    cases = [([o["cost"] * (fac if o["kind"] in COMPUTE else 1) * (gr if o["kind"] == "gat" else 1) for o in ops],
              [[(d, ops[d]["lat"] * (lat if ops[d]["kind"] == "send" else 1) + HOP if w else 0.0)
                for d, w in o["deps"].items()] for o in ops], fac) for gr, fac, lat in CASES]

    def replay(order):
        total = 0.0
        for cost, before, fac in cases:
            free, end = dict((e, 0.0) for e in eng), [0.0] * n
            for i in order:
                t = free[eng[i]]
                for d, w in before[i]:
                    if end[d] + w > t:
                        t = end[d] + w
                end[i] = free[eng[i]] = t + cost[i]
            total += max(end[i] + tail[i] for i in range(n) if tail[i]) / fac
        return total / len(cases)

    zero, tail = [0.0] * n, [o["lat"] if o["kind"] == "store" else 0.0 for o in ops]
    best, r = None, [SEED]

    def draw():
        r[0] = (r[0] * 1103515245 + 12345) % 2147483648
        return r[0] / 2147483648

    for k in range(ROUNDS):
        end, order = place(gap, back, zero, [(-lev[i], i) for i in range(n)])
        length = replay(order)
        if best is None or length < best[0]:
            best = (length, order, end)
        if k % RESTART == RESTART - 1:
            end = best[2]
        lev = place(back, gap, tail, [(-end[i], -i) for i in range(n)])[0]
        for i in range(n):
            lev[i] += SHAKE * draw()
    for k in range(TRIES):
        a, w, s = 135 * draw() - 5, (4, 8, 16)[k % 3], (0.6, 1.6, 4.0)[k // 3 % 3]
        end = [e + s * (draw() + draw() - 1) if a <= e < a + w and o["eng"] != "P" else e for e, o in zip(best[2], ops)]
        if k % 2:
            lev = place(back, gap, tail, [(-end[i], -i) for i in range(n)])[0]
        else:
            lev = [ops[i]["cost"] - end[i] for i in range(n)]
        end, order = place(gap, back, zero, [(-lev[i], i) for i in range(n)])
        length = replay(order)
        if length <= best[0]:
            best = (length, order, end)
    ops[0]["span"] = best[0]
    return best[1]


COMPUTE = ("ts", "tt", "cp", "ms", "scan", "act", "gat", "gtt", "mm", "iota", "sel")


def routes(T, topo):
    chips = sorted(set(topo.chip(c) for c in T.cores))
    ranks = dict((x, [c for c in T.cores if topo.chip(c) == x]) for x in chips)
    out, land = {}, dict(((c, via), []) for c in T.cores for via in (True, False))
    for c in T.cores:
        out[c] = [h for h in topo.cores_of(c) if h not in T.cores and h not in out.values()
                  and topo.die(h) != topo.die(c) and all(topo.may_write(h, d) for d in T.cores)][0]
    for x in chips:
        plane = [y for y in chips if y == x or topo.same_plane(x, y)]
        round_mate = [y for y in chips if y not in plane][plane.index(x)]
        near = [h for h in topo.cores_of(ranks[x][0]) if h not in T.cores and h not in out.values()]
        mate = [h for h in range(NCORES) if topo.mates(topo.chip(h), x) and topo.may_write(h, ranks[x][0])]
        for j, c in enumerate([c for c in T.cores if topo.chip(c) not in (x, round_mate)]):
            land[c, True].append(near[j])
            land[c, False].append(near[j])
        for j, c in enumerate(ranks[round_mate]):
            for via in (True, False):
                land[c, via].append([h for h in mate if topo.die(h) == topo.die(out[c] if via else c)][j])
    return out, land


def fused(g, T, topo, parts):
    g.remote_dma_fused([RemoteDMATransfer(dst_ids=[DstId(rid=topo.addr(d)[0], pnc=topo.addr(d)[1]) for d in ds],
                                          dma_engine_mask=sum(1 << e for e in es), remote_sem=sem, srcs=[ap],
                                          dsts=[ap] * len(ds)) for ds, es, ap, sem in parts], local_sem=T.sem.sent)
    return sum(len(p[1]) for p in parts)


def rank_program(g, core, T, topo):
    out, land = routes(T, topo)
    owner = [c for c in T.cores if core in [c, out[c]] + land[c, True] + land[c, False]]
    if not owner:
        return
    me = owner[0]
    sib = [c for c in T.cores if c != me and topo.chip(c) == topo.chip(me)][0]
    ops = build(T.rank_of(me))
    if not ORDER:
        ORDER.extend(schedule(ops))
    order = ORDER
    outer = topo.engines(me, land[me, False][0])
    inner = [e for e in topo.engines(me, sib) if e not in outer]
    sends = [ops[i]["args"] for i in order if ops[i]["kind"] == "send"]
    total = 0
    if core == out[me]:
        for tab, lo, hi, via, sem, hop in sends:
            if via:
                g.wait_ge(T.sem[hop], len(inner))
                total += fused(g, T, topo, [(land[me, True], outer, T[tab][:, lo:hi], T.sem[hop])])
    elif core != me:
        to = [c for c in T.cores if topo.chip(c) == topo.chip(core) or topo.mates(topo.chip(c), topo.chip(core))]
        eng = topo.engines(core, to[0])
        for j in range(0, len(sends), 2):
            mine = [s for s in sends[j:j + 2] if core in land[me, s[3]]]
            tab, sem = mine[0][0], T.sem[mine[0][4]]
            g.wait_ge(T.sem[mine[0][5]], len(mine) * len(outer))
            if mine[0][2] == mine[-1][1]:
                mine = [(tab, mine[0][1], mine[-1][2])]
            n = len(eng) // len(mine)
            total += fused(g, T, topo, [(to, eng[n * e:n * e + n], T[tab][:, s[1]:s[2]], sem) for e, s in enumerate(mine)])
    if core != me:
        g.wait_ge(T.sem.sent, total)
        return
    arrivals = len(outer) + len(inner)
    for h in set(h for c in T.cores for via in (True, False) for h in land[c, via]):
        if topo.chip(h) == topo.chip(me) or topo.mates(topo.chip(h), topo.chip(me)):
            arrivals += len(topo.engines(h, me))

    pos, cnt, chan = {}, {}, {}
    nd = 0
    for i in order:
        o = ops[i]
        if o["kind"] in COMPUTE:
            chan[i] = o["eng"]
        elif o["kind"] in ("load", "store"):
            chan[i] = "d%d" % nd
            nd += 1
        else:
            chan[i] = o["args"][-1] if o["kind"] == "arr" else None
        cnt[chan[i]] = cnt.get(chan[i], 0) + 1
        pos[i] = cnt[chan[i]]
    known = dict((e, {}) for e in "VSPGYA")
    clock, waits, marked = {}, {}, set()
    where = dict((i, n) for n, i in enumerate(order))
    for i in order:
        o = ops[i]
        kn = known[o["eng"]]
        waits[i] = []
        if o["kind"] != "arr":
            for d in sorted(o["deps"], key=lambda d: -where[d]):
                if o["deps"][d] and kn.get(chan[d], 0) < pos[d]:
                    waits[i].append(d)
                    marked.add(d)
                    for c, v in clock[d].items():
                        if kn.get(c, 0) < v:
                            kn[c] = v
            clock[i] = dict(kn)
        else:
            clock[i] = {}
        clock[i][chan[i]] = pos[i]
    value, run = {}, {}
    for i in order:
        if ops[i]["kind"] in COMPUTE and i in marked:
            run[chan[i]] = run.get(chan[i], 0) + 1
            value[i] = ("c" + chan[i], run[chan[i]])
        elif ops[i]["kind"] in ("load", "store"):
            value[i] = (chan[i], 16)
        elif ops[i]["kind"] == "arr":
            value[i] = (chan[i], arrivals * len(ops[i]["deps"]) // 2)

    Q = {"V": g.vector, "S": g.scalar, "P": g.tensor, "G": g, "Y": g.sync}

    def ap(x):
        return T[x[0]][x[1]] if isinstance(x, tuple) else x

    for i in order:
        o = ops[i]
        k, a = o["kind"], o["args"]
        if k == "arr":
            continue
        q = Q[o["eng"]]
        for d in waits[i]:
            q.wait_ge(T.sem[value[d][0]], value[d][1])
        if k == "send":
            tab, lo, hi, via, sem, hop = a
            a, s, h = T[tab][:, lo:hi], T.sem[sem], T.sem[hop]
            if via:
                total += fused(g, T, topo, [([out[me]], inner, a, h), ([sib], outer, a, s)])
            else:
                total += fused(g, T, topo, [(land[me, False], outer, a, h), ([sib], inner, a, s)])
            continue
        if k == "ts":
            ins = (q.tensor_scalar(ap(a[0]), ap(a[1]), ap(a[2]), None, a[4]) if a[5] is None
                   else q.tensor_scalar(ap(a[0]), ap(a[1]), ap(a[2]), ap(a[3]), a[4], a[5]))
        elif k == "tt":
            ins = q.tensor_tensor(ap(a[0]), ap(a[1]), ap(a[2]), a[3])
        elif k == "cp":
            ins = q.tensor_copy(ap(a[0]), ap(a[1]))
        elif k == "ms":
            ins = q.memset(ap(a[0]), a[1])
        elif k == "scan":
            ins = q.tensor_tensor_scan(ap(a[0]), ap(a[1]), ap(a[2]), 0.0, ALU.mult, ALU.add)
        elif k == "act":
            ins = q.activation(ap(a[0]), ap(a[1]), a[2], bias=ap(a[3]), scale=ap(a[4]))
        elif k == "gat":
            src = ap(a[1]).indirect(ap(a[2]))
            ins = q.tensor_copy(ap(a[0]), src) if o["eng"] == "V" else q.activation(ap(a[0]), src, ACT.Copy)
        elif k == "gtt":
            ins = q.tensor_tensor(ap(a[0]), ap(a[1]).indirect(ap(a[2])), ap(a[3]), ALU.mult)
        elif k == "mm":
            ins = q.matmul(ap(a[0]), ap(a[1]), ap(a[2]), a[3], a[4])
        elif k == "iota":
            ins = (q.iota(ap(a[0]), a[1], a[2], a[3], allow_small_or_imprecise_dtypes=True) if a[4]
                   else q.iota(ap(a[0]), a[1], a[2], a[3]))
        elif k == "sel":
            ins = q.affine_select(ap(a[0]), ap(a[1]), a[2], a[3], a[4], a[5], a[6])
        elif k == "load":
            ins = q.dma_start(ap(a[0]), T[a[1]][:, a[2]:a[3]])
        else:
            ins = q.dma_start(T[a[1]][:, a[2]:a[3]], ap(a[0]))
        if i in value:
            ins.then_inc(T.sem[value[i][0]], value[i][1] if k in ("load", "store") else 1)
    for i in order:
        if ops[i]["kind"] == "store":
            g.sync.wait_ge(T.sem[value[i][0]], 16)
    g.wait_ge(T.sem.sent, total)
